import numpy as np
import ml_dtypes


def mxq(x, axis, fmt="e4m3"):
    dtype, down = {"e4m3": (ml_dtypes.float8_e4m3fn, 7), "e5m2": (ml_dtypes.float8_e5m2, 14)}[fmt]
    v = np.moveaxis(np.asarray(x, np.float32).astype(ml_dtypes.bfloat16).astype(np.float64), axis, -1)
    blocks = v.reshape(v.shape[:-1] + (-1, 32))
    amax = np.abs(blocks).max(-1, keepdims=True)
    byte = np.maximum(np.where(amax > 0, np.frexp(amax)[1] - 1 + 127, 0) - down, 1)
    scale = np.exp2(byte - 127.0)
    codes = (blocks / scale).astype(np.float32).astype(dtype).astype(np.float64)
    return np.moveaxis((codes * scale).reshape(v.shape), -1, axis)


WIDE = False


def mx_kscale(k):
    if not WIDE:
        return np.ones(k)
    levels = np.array([10, -10, 5, -5, 0])
    if k % 512:
        return np.exp2(np.random.permutation(np.resize(levels, k // 32))).repeat(32)
    a = np.empty((k // 512, 16))
    for p in range(k // 512):
        a[p, :8] = np.random.permutation(np.resize(levels, 8))
        for g in range(8):
            far = levels[np.abs(levels - a[p, g]) >= 10]
            a[p, g + 8] = far[np.random.randint(len(far))]
    return np.exp2(a.ravel()).repeat(32)


def f64(x):
    return np.asarray(x).astype(np.float64)


def striped(idx):
    return np.tile(idx.reshape(-1, 16).T, (8, 1)).astype(np.uint16)


def unstriped(offs):
    return offs[:16].T.reshape(-1).astype(np.int64)


K, T, E, C, N = 1024, 512, 4, 256, 256


def by_expert(wq, xq):
    return np.concatenate([wq[e].T @ xq[:, e * C:(e + 1) * C] for e in range(E)], axis=1)


def setup_inputs():
    n = np.random.standard_normal
    s = mx_kscale(K)[:, None]
    first = np.random.permutation(np.repeat(np.arange(E), T // E))
    second = (first + 1 + np.random.permutation(np.repeat(np.arange(E - 1), -(-T // (E - 1)))[:T])) % E
    while np.bincount(second, minlength=E).max() != T // E:
        load = np.bincount(second, minlength=E); hi, lo = int(load.argmax()), int(load.argmin())
        t = np.flatnonzero((second == hi) & (first != lo))[0]; second[t] = lo
    slot_token = np.empty(E * C, np.int64); pos = np.empty((2, T), np.int64); fill = np.zeros(E, np.int64)
    place = np.stack([np.random.permutation(C) for _ in range(E)])
    for r, deal in enumerate((first, second)):
        for t in np.random.permutation(T):
            e = deal[t]; j = e * C + place[e, fill[e]]; fill[e] += 1; slot_token[j] = t; pos[r, t] = j
    g = np.random.uniform(0.2, 0.8, T)
    return {
        "xT": (n((K, T)) * s).astype(np.float32),
        "w": (n((E, K, N)) / np.sqrt(K) / s[None]).astype(np.float32),
        "gate": np.stack([np.tile(g, (N, 1)), np.tile(1.0 - g, (N, 1))]).astype(np.float32),
        "offs": striped(slot_token),
        "pos1": striped(pos[0]),
        "pos2": striped(pos[1]),
    }


def reference(xT, w, gate, offs, pos1, pos2):
    idx = unstriped(offs)
    xq = mxq(f64(xT)[:, idx], 0, "e4m3")
    y = by_expert(mxq(f64(w), 1, "e4m3"), xq)
    return f64(gate[0]) * y[:, unstriped(pos1)] + f64(gate[1]) * y[:, unstriped(pos2)]

@@ -1,0 +1,164 @@
+from contextlib import ExitStack
+
+import concourse.mybir as mybir
+
+K, T, E, C, N = 1024, 512, 4, 256, 256
+FLOPS = 2 * K * N * E * C
+
+F32 = mybir.dt.float32
+BF16 = mybir.dt.bfloat16
+U32 = mybir.dt.uint32
+U16 = mybir.dt.uint16
+U8 = mybir.dt.uint8
+FP8X4 = mybir.dt.float8_e4m3fn_x4
+MULT = mybir.AluOpType.mult
+ADD = mybir.AluOpType.add
+COPY = mybir.ActivationFunctionType.Copy
+
+P = 128
+PACK = 4
+K_PASS = P * PACK
+PASSES = K // K_PASS
+BLOCKS = N // P
+
+F_PASSES = []
+B_PASSES = []
+X_ENG = ["S","S","S","S","S","S","S","S"]
+W_ENG = ["S","S","S","S","S","S","S","S"]
+G4_BUFS = 3
+FAST = False
+
+
+def tile_routed_moe_kernel(tc, xT, w, gate, offs, pos1, pos2, out):
+    nc = tc.nc
+    engines = {"S": nc.scalar, "V": nc.vector, "G": nc.gpsimd}
+
+    def move(eng, dst, src):
+        if eng == "S":
+            nc.scalar.copy(dst, src)
+        else:
+            engines[eng].tensor_copy(dst, src)
+
+    def interleave(eng, dst, src):
+        if FAST:
+            move(eng, dst.rearrange("p (c i) t -> p c t i", i=4), src.rearrange("p t (c i) -> p c t i", i=4))
+        else:
+            move(eng, dst, src.rearrange("p t c -> p c t"))
+
+    with ExitStack() as ctx:
+        lists = ctx.enter_context(tc.tile_pool(name="lists", bufs=1))
+        keep = ctx.enter_context(tc.tile_pool(name="keep", bufs=1))
+        ring = ctx.enter_context(tc.tile_pool(name="ring", bufs=G4_BUFS))
+        psum = ctx.enter_context(tc.psum_pool(name="psum", bufs=1))
+
+        offs_t = lists.tile([P, E * C // 16], U16, name="offs_t")
+        nc.sync.dma_start(offs_t[:], offs)
+
+        x_view = xT.rearrange("(g p t) n -> g p t n", p=P, t=PACK)
+        planes = {}
+        raws = {}
+        order = [[0,0],[0,1],[0,2],[0,3],[1,0],[1,1],[1,2],[1,3]]
+        for g, t in order:
+            if g in F_PASSES or g in B_PASSES:
+                if g not in raws:
+                    raws[g] = keep.tile([P, PACK, T], F32, name="raw%d" % g)
+                nc.sync.dma_start(raws[g][:, t, :], x_view[g, :, t, :])
+            else:
+                plane = keep.tile([P, T], F32, name="plane%d_%d" % (g, t))
+                nc.sync.dma_start(plane[:], x_view[g, :, t, :])
+                planes[(g, t)] = plane
+
+        w_raw = {}
+        for e in range(E):
+            for g in range(PASSES):
+                raw = keep.tile([P, PACK, N], F32, name="w_raw%d_%d" % (e, g))
+                nc.sync.dma_start(
+                    raw[:], w[e, g * K_PASS : (g + 1) * K_PASS, :].rearrange("(p j) n -> p j n", j=PACK)
+                )
+                w_raw[(e, g)] = raw
+
+        pos1_t = lists.tile([P, T // 16], U16, name="pos1_t")
+        nc.sync.dma_start(pos1_t[:], pos1)
+        pos2_t = lists.tile([P, T // 16], U16, name="pos2_t")
+        nc.sync.dma_start(pos2_t[:], pos2)
+        pos_t = (pos1_t, pos2_t)
+
+        gate_t = {}
+        for m in range(BLOCKS):
+            for r in range(2):
+                gt = keep.tile([P, T], F32, name="gate%d_%d" % (r, m))
+                nc.sync.dma_start(gt[:], gate[r, m * P : (m + 1) * P, :])
+                gate_t[(r, m)] = gt
+
+        xbf = {}
+        for g in F_PASSES:
+            xbf[g] = keep.tile([P, PACK, T], BF16, name="xbf%d" % g)
+            for t in range(PACK):
+                nc.scalar.copy(xbf[g][:, t, :], raws[g][:, t, :])
+
+        y_sb = [keep.tile([P, E * C], F32, name="y_sb%d" % m) for m in range(BLOCKS)]
+
+        cols = C // 16
+        for e in range(E):
+            x_codes, x_scales, w_codes, w_scales = {}, {}, {}, {}
+            my_offs = offs_t[:, e * cols : (e + 1) * cols]
+            xbs = {}
+            for g in range(PASSES):
+                xb = keep.tile([P, C, PACK], BF16, name="xb%d_%d" % (e, g), align_bytes=64)
+                xbs[g] = xb
+                if g in F_PASSES:
+                    for t in range(PACK):
+                        nc.scalar.activation(xb[:, :, t], xbf[g][:, t, :].indirect(my_offs), COPY)
+                elif g in B_PASSES:
+                    for t in range(PACK):
+                        nc.vector.tensor_copy(xb[:, :, t], raws[g][:, t, :].indirect(my_offs))
+                else:
+                    g4 = ring.tile([P, PACK, C], F32, name="g4")
+                    for t in range(PACK):
+                        nc.vector.tensor_copy(g4[:, t, :], planes[(g, t)][:].indirect(my_offs))
+                    interleave(X_ENG[e * PASSES + g], xb[:], g4[:])
+            for g in range(PASSES):
+                xc = keep.tile([P, C], U32, name="xc%d_%d" % (e, g), align_bytes=64)
+                xs = keep.tile([P, C], U8, name="xs%d_%d" % (e, g), align_bytes=64)
+                nc.vector.quantize_mx(
+                    out=xc[:].bitcast(FP8X4), scales=xs[:], in_=xbs[g][:].rearrange("p c t -> p (c t)")
+                )
+                x_codes[g], x_scales[g] = xc, xs
+
+            wb = keep.tile([P, PASSES, N, PACK], BF16, name="wb%d" % e, align_bytes=64)
+            for g in range(PASSES):
+                interleave(W_ENG[e * PASSES + g], wb[:, g, :, :], w_raw[(e, g)][:])
+            wc = keep.tile([P, PASSES, N], U32, name="wc%d" % e, align_bytes=64)
+            ws = keep.tile([P, PASSES, N], U8, name="ws%d" % e, align_bytes=64)
+            nc.vector.quantize_mx(
+                out=wc[:].rearrange("p g n -> p (g n)").bitcast(FP8X4),
+                scales=ws[:].rearrange("p g n -> p (g n)"),
+                in_=wb[:].rearrange("p g n j -> p (g n j)"),
+            )
+
+            for m in range(BLOCKS):
+                acc = psum.tile([P, C], F32, name="acc%d_%d" % (e, m))
+                for g in range(PASSES):
+                    nc.tensor.matmul_mx(
+                        out=acc[:],
+                        lhsT=wc[:, g, m * P : (m + 1) * P].bitcast(FP8X4),
+                        lhsT_scale=ws[:, g, m * P : (m + 1) * P],
+                        rhs=x_codes[g][:].bitcast(FP8X4),
+                        rhs_scale=x_scales[g][:],
+                        start=(g == 0),
+                        stop=(g == PASSES - 1),
+                    )
+                if e == E - 1 and m == 0:
+                    nc.vector.tensor_copy(y_sb[m][:, e * C : (e + 1) * C], acc[:])
+                else:
+                    nc.scalar.copy(y_sb[m][:, e * C : (e + 1) * C], acc[:])
+
+        for m in range(BLOCKS):
+            parts = []
+            for r in range(2):
+                part = keep.tile([P, T], F32, name="part%d_%d" % (r, m))
+                nc.vector.tensor_tensor(part[:], y_sb[m][:].indirect(pos_t[r][:]), gate_t[(r, m)][:], MULT)
+                parts.append(part)
+            res = keep.tile([P, T], F32, name="res%d" % m)
+            nc.vector.tensor_tensor(res[:], parts[0][:], parts[1][:], ADD)
+            nc.sync.dma_start(out[m * P : (m + 1) * P, :], res[:])

@@ -21,12 +21,12 @@ K_PASS = P * PACK
 PASSES = K // K_PASS
 BLOCKS = N // P
 
-F_PASSES = []
-B_PASSES = []
-X_ENG = ["S","S","S","S","S","S","S","S"]
-W_ENG = ["S","S","S","S","S","S","S","S"]
-G4_BUFS = 3
-FAST = False
+V_FORM = "a"
+X_ENG = ["V","V","V","V"]
+W_ENG = ["V","V","V","V"]
+G4_BUFS = 4
+SPLIT_LAST = True
+TEXT = "tokens_first"
 
 
 def tile_routed_moe_kernel(tc, xT, w, gate, offs, pos1, pos2, out):
@@ -39,12 +39,6 @@ def tile_routed_moe_kernel(tc, xT, w, gate, offs, pos1, pos2, out):
         else:
             engines[eng].tensor_copy(dst, src)
 
-    def interleave(eng, dst, src):
-        if FAST:
-            move(eng, dst.rearrange("p (c i) t -> p c t i", i=4), src.rearrange("p t (c i) -> p c t i", i=4))
-        else:
-            move(eng, dst, src.rearrange("p t c -> p c t"))
-
     with ExitStack() as ctx:
         lists = ctx.enter_context(tc.tile_pool(name="lists", bufs=1))
         keep = ctx.enter_context(tc.tile_pool(name="keep", bufs=1))
@@ -56,26 +50,27 @@ def tile_routed_moe_kernel(tc, xT, w, gate, offs, pos1, pos2, out):
 
         x_view = xT.rearrange("(g p t) n -> g p t n", p=P, t=PACK)
         planes = {}
-        raws = {}
-        order = [[0,0],[0,1],[0,2],[0,3],[1,0],[1,1],[1,2],[1,3]]
-        for g, t in order:
-            if g in F_PASSES or g in B_PASSES:
-                if g not in raws:
-                    raws[g] = keep.tile([P, PACK, T], F32, name="raw%d" % g)
-                nc.sync.dma_start(raws[g][:, t, :], x_view[g, :, t, :])
+        raw1 = keep.tile([P, PACK, T], F32, name="raw1")
+        raw0 = None
+        if V_FORM == "b":
+            raw0 = keep.tile([P, PACK, T], F32, name="raw0")
+        for t in range(PACK):
+            if V_FORM == "b":
+                nc.sync.dma_start(raw0[:, t, :], x_view[0, :, t, :])
             else:
-                plane = keep.tile([P, T], F32, name="plane%d_%d" % (g, t))
-                nc.sync.dma_start(plane[:], x_view[g, :, t, :])
-                planes[(g, t)] = plane
+                plane = keep.tile([P, T], F32, name="plane%d" % t)
+                nc.sync.dma_start(plane[:], x_view[0, :, t, :])
+                planes[t] = plane
+            nc.sync.dma_start(raw1[:, t, :], x_view[1, :, t, :])
 
         w_raw = {}
         for e in range(E):
+            raw = keep.tile([P, PASSES, PACK, N], F32, name="w_raw%d" % e)
             for g in range(PASSES):
-                raw = keep.tile([P, PACK, N], F32, name="w_raw%d_%d" % (e, g))
                 nc.sync.dma_start(
-                    raw[:], w[e, g * K_PASS : (g + 1) * K_PASS, :].rearrange("(p j) n -> p j n", j=PACK)
+                    raw[:, g, :, :], w[e, g * K_PASS : (g + 1) * K_PASS, :].rearrange("(p j) n -> p j n", j=PACK)
                 )
-                w_raw[(e, g)] = raw
+            w_raw[e] = raw
 
         pos1_t = lists.tile([P, T // 16], U16, name="pos1_t")
         nc.sync.dma_start(pos1_t[:], pos1)
@@ -90,68 +85,87 @@ def tile_routed_moe_kernel(tc, xT, w, gate, offs, pos1, pos2, out):
                 nc.sync.dma_start(gt[:], gate[r, m * P : (m + 1) * P, :])
                 gate_t[(r, m)] = gt
 
-        xbf = {}
-        for g in F_PASSES:
-            xbf[g] = keep.tile([P, PACK, T], BF16, name="xbf%d" % g)
-            for t in range(PACK):
-                nc.scalar.copy(xbf[g][:, t, :], raws[g][:, t, :])
+        xbf = keep.tile([P, PACK, T], BF16, name="xbf")
+        for t in range(PACK):
+            nc.scalar.copy(xbf[:, t, :], raw1[:, t, :])
 
         y_sb = [keep.tile([P, E * C], F32, name="y_sb%d" % m) for m in range(BLOCKS)]
 
         cols = C // 16
-        for e in range(E):
-            x_codes, x_scales, w_codes, w_scales = {}, {}, {}, {}
-            my_offs = offs_t[:, e * cols : (e + 1) * cols]
-            xbs = {}
-            for g in range(PASSES):
-                xb = keep.tile([P, C, PACK], BF16, name="xb%d_%d" % (e, g), align_bytes=64)
-                xbs[g] = xb
-                if g in F_PASSES:
-                    for t in range(PACK):
-                        nc.scalar.activation(xb[:, :, t], xbf[g][:, t, :].indirect(my_offs), COPY)
-                elif g in B_PASSES:
-                    for t in range(PACK):
-                        nc.vector.tensor_copy(xb[:, :, t], raws[g][:, t, :].indirect(my_offs))
-                else:
-                    g4 = ring.tile([P, PACK, C], F32, name="g4")
-                    for t in range(PACK):
-                        nc.vector.tensor_copy(g4[:, t, :], planes[(g, t)][:].indirect(my_offs))
-                    interleave(X_ENG[e * PASSES + g], xb[:], g4[:])
-            for g in range(PASSES):
-                xc = keep.tile([P, C], U32, name="xc%d_%d" % (e, g), align_bytes=64)
-                xs = keep.tile([P, C], U8, name="xs%d_%d" % (e, g), align_bytes=64)
-                nc.vector.quantize_mx(
-                    out=xc[:].bitcast(FP8X4), scales=xs[:], in_=xbs[g][:].rearrange("p c t -> p (c t)")
-                )
-                x_codes[g], x_scales[g] = xc, xs
+        xc, xs, wc, ws = {}, {}, {}, {}
 
-            wb = keep.tile([P, PASSES, N, PACK], BF16, name="wb%d" % e, align_bytes=64)
-            for g in range(PASSES):
-                interleave(W_ENG[e * PASSES + g], wb[:, g, :, :], w_raw[(e, g)][:])
-            wc = keep.tile([P, PASSES, N], U32, name="wc%d" % e, align_bytes=64)
-            ws = keep.tile([P, PASSES, N], U8, name="ws%d" % e, align_bytes=64)
+        def tokens(e):
+            my_offs = offs_t[:, e * cols : (e + 1) * cols]
+            xb = keep.tile([P, PASSES, C, PACK], BF16, name="xb%d" % e, align_bytes=64)
+            if V_FORM == "b":
+                for t in range(PACK):
+                    nc.vector.tensor_copy(xb[:, 0, :, t], raw0[:, t, :].indirect(my_offs))
+            else:
+                g4 = ring.tile([P, PACK, C], F32, name="g4")
+                for t in range(PACK):
+                    nc.vector.tensor_copy(g4[:, t, :], planes[t][:].indirect(my_offs))
+                move(X_ENG[e], xb[:, 0, :, :], g4[:].rearrange("p t c -> p c t"))
+            for t in range(PACK):
+                nc.scalar.activation(xb[:, 1, :, t], xbf[:, t, :].indirect(my_offs), COPY)
+            xc[e] = keep.tile([P, PASSES, C], U32, name="xc%d" % e, align_bytes=64)
+            xs[e] = keep.tile([P, PASSES, C], U8, name="xs%d" % e, align_bytes=64)
             nc.vector.quantize_mx(
-                out=wc[:].rearrange("p g n -> p (g n)").bitcast(FP8X4),
-                scales=ws[:].rearrange("p g n -> p (g n)"),
-                in_=wb[:].rearrange("p g n j -> p (g n j)"),
+                out=xc[e][:].rearrange("p g c -> p (g c)").bitcast(FP8X4),
+                scales=xs[e][:].rearrange("p g c -> p (g c)"),
+                in_=xb[:].rearrange("p g c t -> p (g c t)"),
             )
 
-            for m in range(BLOCKS):
-                acc = psum.tile([P, C], F32, name="acc%d_%d" % (e, m))
+        def weights(e):
+            wb = keep.tile([P, PASSES, N, PACK], BF16, name="wb%d" % e, align_bytes=64)
+            wc[e] = keep.tile([P, PASSES, N], U32, name="wc%d" % e, align_bytes=64)
+            ws[e] = keep.tile([P, PASSES, N], U8, name="ws%d" % e, align_bytes=64)
+            if SPLIT_LAST and e == E - 1:
                 for g in range(PASSES):
+                    move(W_ENG[e], wb[:, g, :, :], w_raw[e][:, g, :, :].rearrange("p j n -> p n j"))
+                for g in range(PASSES):
+                    nc.vector.quantize_mx(
+                        out=wc[e][:, g, :].bitcast(FP8X4),
+                        scales=ws[e][:, g, :],
+                        in_=wb[:, g, :, :].rearrange("p n j -> p (n j)"),
+                    )
+            else:
+                move(W_ENG[e], wb[:], w_raw[e][:].rearrange("p g j n -> p g n j"))
+                nc.vector.quantize_mx(
+                    out=wc[e][:].rearrange("p g n -> p (g n)").bitcast(FP8X4),
+                    scales=ws[e][:].rearrange("p g n -> p (g n)"),
+                    in_=wb[:].rearrange("p g n j -> p (g n j)"),
+                )
+
+        def multiply(e):
+            accs = [psum.tile([P, C], F32, name="acc%d_%d" % (e, m)) for m in range(BLOCKS)]
+            for g in range(PASSES):
+                for m in range(BLOCKS):
                     nc.tensor.matmul_mx(
-                        out=acc[:],
-                        lhsT=wc[:, g, m * P : (m + 1) * P].bitcast(FP8X4),
-                        lhsT_scale=ws[:, g, m * P : (m + 1) * P],
-                        rhs=x_codes[g][:].bitcast(FP8X4),
-                        rhs_scale=x_scales[g][:],
+                        out=accs[m][:],
+                        lhsT=wc[e][:, g, m * P : (m + 1) * P].bitcast(FP8X4),
+                        lhsT_scale=ws[e][:, g, m * P : (m + 1) * P],
+                        rhs=xc[e][:, g, :].bitcast(FP8X4),
+                        rhs_scale=xs[e][:, g, :],
                         start=(g == 0),
                         stop=(g == PASSES - 1),
                     )
+            for m in range(BLOCKS):
                 if e == E - 1 and m == 0:
-                    nc.vector.tensor_copy(y_sb[m][:, e * C : (e + 1) * C], acc[:])
+                    nc.vector.tensor_copy(y_sb[m][:, e * C : (e + 1) * C], accs[m][:])
                 else:
-                    nc.scalar.copy(y_sb[m][:, e * C : (e + 1) * C], acc[:])
+                    nc.scalar.copy(y_sb[m][:, e * C : (e + 1) * C], accs[m][:])
+
+        if TEXT == "tokens_first":
+            for e in range(E):
+                tokens(e)
+            for e in range(E):
+                weights(e)
+                multiply(e)
+        else:
+            for e in range(E):
+                tokens(e)
+                weights(e)
+                multiply(e)
 
         for m in range(BLOCKS):
             parts = []

@@ -21,12 +21,10 @@ K_PASS = P * PACK
 PASSES = K // K_PASS
 BLOCKS = N // P
 
-V_FORM = "a"
+V_FORM = "b"
 X_ENG = ["V","V","V","V"]
-W_ENG = ["V","V","V","V"]
-G4_BUFS = 4
-SPLIT_LAST = True
-TEXT = "tokens_first"
+W_GROUPS = [[0,0,2,"V","wa"],[0,2,2,"V","wbb"],[1,0,2,"V","stage2"],[1,2,2,"V","stage3"]]
+Y_ENG = ["S","S","S","S","S","S","S","S"]
 
 
 def tile_routed_moe_kernel(tc, xT, w, gate, offs, pos1, pos2, out):
@@ -42,7 +40,6 @@ def tile_routed_moe_kernel(tc, xT, w, gate, offs, pos1, pos2, out):
     with ExitStack() as ctx:
         lists = ctx.enter_context(tc.tile_pool(name="lists", bufs=1))
         keep = ctx.enter_context(tc.tile_pool(name="keep", bufs=1))
-        ring = ctx.enter_context(tc.tile_pool(name="ring", bufs=G4_BUFS))
         psum = ctx.enter_context(tc.psum_pool(name="psum", bufs=1))
 
         offs_t = lists.tile([P, E * C // 16], U16, name="offs_t")
@@ -63,14 +60,13 @@ def tile_routed_moe_kernel(tc, xT, w, gate, offs, pos1, pos2, out):
                 planes[t] = plane
             nc.sync.dma_start(raw1[:, t, :], x_view[1, :, t, :])
 
-        w_raw = {}
+        w_raw = keep.tile([P, E * PASSES, PACK, N], F32, name="w_raw")
         for e in range(E):
-            raw = keep.tile([P, PASSES, PACK, N], F32, name="w_raw%d" % e)
             for g in range(PASSES):
                 nc.sync.dma_start(
-                    raw[:, g, :, :], w[e, g * K_PASS : (g + 1) * K_PASS, :].rearrange("(p j) n -> p j n", j=PACK)
+                    w_raw[:, e * PASSES + g, :, :],
+                    w[e, g * K_PASS : (g + 1) * K_PASS, :].rearrange("(p j) n -> p j n", j=PACK),
                 )
-            w_raw[e] = raw
 
         pos1_t = lists.tile([P, T // 16], U16, name="pos1_t")
         nc.sync.dma_start(pos1_t[:], pos1)
@@ -92,80 +88,82 @@ def tile_routed_moe_kernel(tc, xT, w, gate, offs, pos1, pos2, out):
         y_sb = [keep.tile([P, E * C], F32, name="y_sb%d" % m) for m in range(BLOCKS)]
 
         cols = C // 16
-        xc, xs, wc, ws = {}, {}, {}, {}
+        xb = [keep.tile([P, PASSES, C, PACK], BF16, name="xb%d" % e, tag="stage%d" % e, align_bytes=64) for e in range(E)]
+        xc = {}
+        xs = [keep.tile([P, PASSES, C], U8, name="xs%d" % e, align_bytes=64) for e in range(E)]
 
-        def tokens(e):
+        g4s = {}
+        for e in range(E):
             my_offs = offs_t[:, e * cols : (e + 1) * cols]
-            xb = keep.tile([P, PASSES, C, PACK], BF16, name="xb%d" % e, align_bytes=64)
             if V_FORM == "b":
                 for t in range(PACK):
-                    nc.vector.tensor_copy(xb[:, 0, :, t], raw0[:, t, :].indirect(my_offs))
+                    nc.vector.tensor_copy(xb[e][:, 0, :, t], raw0[:, t, :].indirect(my_offs))
             else:
-                g4 = ring.tile([P, PACK, C], F32, name="g4")
+                g4 = keep.tile([P, PACK, C], F32, name="g4_%d" % e)
                 for t in range(PACK):
                     nc.vector.tensor_copy(g4[:, t, :], planes[t][:].indirect(my_offs))
-                move(X_ENG[e], xb[:, 0, :, :], g4[:].rearrange("p t c -> p c t"))
+                g4s[e] = g4
             for t in range(PACK):
-                nc.scalar.activation(xb[:, 1, :, t], xbf[:, t, :].indirect(my_offs), COPY)
-            xc[e] = keep.tile([P, PASSES, C], U32, name="xc%d" % e, align_bytes=64)
-            xs[e] = keep.tile([P, PASSES, C], U8, name="xs%d" % e, align_bytes=64)
+                nc.scalar.activation(xb[e][:, 1, :, t], xbf[:, t, :].indirect(my_offs), COPY)
+        if V_FORM == "a":
+            for e in range(E):
+                move(X_ENG[e], xb[e][:, 0, :, :], g4s[e][:].rearrange("p t c -> p c t"))
+
+        wbs, wcs, wss = {}, {}, {}
+
+        def lay(i):
+            m, e0, ne, eng, tag = W_GROUPS[i]
+            u = ne * PASSES
+            wbs[i] = keep.tile([P, u, P, PACK], BF16, name="wb%d" % i, tag=tag, align_bytes=64)
+            move(
+                eng,
+                wbs[i][:],
+                w_raw[:, e0 * PASSES : e0 * PASSES + u, :, m * P : (m + 1) * P].rearrange("p u j n -> p u n j"),
+            )
+
+        def quant_w(i):
+            m, e0, ne, eng, tag = W_GROUPS[i]
+            u = ne * PASSES
+            wcs[i] = keep.tile([P, u, P], U32, name="wc%d" % i, align_bytes=64)
+            wss[i] = keep.tile([P, u, P], U8, name="ws%d" % i, align_bytes=64)
+            nc.vector.quantize_mx(
+                out=wcs[i][:].rearrange("p u n -> p (u n)").bitcast(FP8X4),
+                scales=wss[i][:].rearrange("p u n -> p (u n)"),
+                in_=wbs[i][:].rearrange("p u n j -> p (u n j)"),
+            )
+
+        lay(0)
+        lay(1)
+        quant_w(0)
+        quant_w(1)
+        XC_TAGS = ["wa","wbb","stage0","stage1"]
+        for e in range(E):
+            xc[e] = keep.tile([P, PASSES, C], U32, name="xc%d" % e, tag=XC_TAGS[e], align_bytes=64)
             nc.vector.quantize_mx(
                 out=xc[e][:].rearrange("p g c -> p (g c)").bitcast(FP8X4),
                 scales=xs[e][:].rearrange("p g c -> p (g c)"),
-                in_=xb[:].rearrange("p g c t -> p (g c t)"),
+                in_=xb[e][:].rearrange("p g c t -> p (g c t)"),
             )
+        lay(2)
+        lay(3)
+        quant_w(2)
+        quant_w(3)
 
-        def weights(e):
-            wb = keep.tile([P, PASSES, N, PACK], BF16, name="wb%d" % e, align_bytes=64)
-            wc[e] = keep.tile([P, PASSES, N], U32, name="wc%d" % e, align_bytes=64)
-            ws[e] = keep.tile([P, PASSES, N], U8, name="ws%d" % e, align_bytes=64)
-            if SPLIT_LAST and e == E - 1:
+        for i, (m, e0, ne, eng, tag) in enumerate(W_GROUPS):
+            wc, ws = wcs[i], wss[i]
+            for e in range(e0, e0 + ne):
+                acc = psum.tile([P, C], F32, name="acc%d_%d" % (e, m))
                 for g in range(PASSES):
-                    move(W_ENG[e], wb[:, g, :, :], w_raw[e][:, g, :, :].rearrange("p j n -> p n j"))
-                for g in range(PASSES):
-                    nc.vector.quantize_mx(
-                        out=wc[e][:, g, :].bitcast(FP8X4),
-                        scales=ws[e][:, g, :],
-                        in_=wb[:, g, :, :].rearrange("p n j -> p (n j)"),
-                    )
-            else:
-                move(W_ENG[e], wb[:], w_raw[e][:].rearrange("p g j n -> p g n j"))
-                nc.vector.quantize_mx(
-                    out=wc[e][:].rearrange("p g n -> p (g n)").bitcast(FP8X4),
-                    scales=ws[e][:].rearrange("p g n -> p (g n)"),
-                    in_=wb[:].rearrange("p g n j -> p (g n j)"),
-                )
-
-        def multiply(e):
-            accs = [psum.tile([P, C], F32, name="acc%d_%d" % (e, m)) for m in range(BLOCKS)]
-            for g in range(PASSES):
-                for m in range(BLOCKS):
                     nc.tensor.matmul_mx(
-                        out=accs[m][:],
-                        lhsT=wc[e][:, g, m * P : (m + 1) * P].bitcast(FP8X4),
-                        lhsT_scale=ws[e][:, g, m * P : (m + 1) * P],
+                        out=acc[:],
+                        lhsT=wc[:, (e - e0) * PASSES + g, :].bitcast(FP8X4),
+                        lhsT_scale=ws[:, (e - e0) * PASSES + g, :],
                         rhs=xc[e][:, g, :].bitcast(FP8X4),
                         rhs_scale=xs[e][:, g, :],
                         start=(g == 0),
                         stop=(g == PASSES - 1),
                     )
-            for m in range(BLOCKS):
-                if e == E - 1 and m == 0:
-                    nc.vector.tensor_copy(y_sb[m][:, e * C : (e + 1) * C], accs[m][:])
-                else:
-                    nc.scalar.copy(y_sb[m][:, e * C : (e + 1) * C], accs[m][:])
-
-        if TEXT == "tokens_first":
-            for e in range(E):
-                tokens(e)
-            for e in range(E):
-                weights(e)
-                multiply(e)
-        else:
-            for e in range(E):
-                tokens(e)
-                weights(e)
-                multiply(e)
+                move(Y_ENG[m * E + e], y_sb[m][:, e * C : (e + 1) * C], acc[:])
 
         for m in range(BLOCKS):
             parts = []

@@ -21,10 +21,12 @@ K_PASS = P * PACK
 PASSES = K // K_PASS
 BLOCKS = N // P
 
-V_FORM = "b"
 X_ENG = ["V","V","V","V"]
-W_GROUPS = [[0,0,2,"V","wa"],[0,2,2,"V","wbb"],[1,0,2,"V","stage2"],[1,2,2,"V","stage3"]]
+W_GROUPS = [[0,0,2,"wa",["V","V"]],[0,2,2,"wbb",["V","V"]],[1,0,2,"stage2",["V","V"]],[1,2,2,"xbf",["S","S"]]]
+WC_TAGS = ["wc0","wc1","wc2","stage3"]
+XC_TAGS = ["wa","wbb","stage0","stage1"]
 Y_ENG = ["S","S","S","S","S","S","S","S"]
+LOADS = [["p",0],["r",0],["p",1],["r",1],["p",2],["r",2],["p",3],["r",3],["w",0],["w",1],["w",2],["w",3]]
 
 
 def tile_routed_moe_kernel(tc, xT, w, gate, offs, pos1, pos2, out):
@@ -46,27 +48,20 @@ def tile_routed_moe_kernel(tc, xT, w, gate, offs, pos1, pos2, out):
         nc.sync.dma_start(offs_t[:], offs)
 
         x_view = xT.rearrange("(g p t) n -> g p t n", p=P, t=PACK)
-        planes = {}
+        planes = [keep.tile([P, T], F32, name="plane%d" % t) for t in range(PACK)]
         raw1 = keep.tile([P, PACK, T], F32, name="raw1")
-        raw0 = None
-        if V_FORM == "b":
-            raw0 = keep.tile([P, PACK, T], F32, name="raw0")
-        for t in range(PACK):
-            if V_FORM == "b":
-                nc.sync.dma_start(raw0[:, t, :], x_view[0, :, t, :])
-            else:
-                plane = keep.tile([P, T], F32, name="plane%d" % t)
-                nc.sync.dma_start(plane[:], x_view[0, :, t, :])
-                planes[t] = plane
-            nc.sync.dma_start(raw1[:, t, :], x_view[1, :, t, :])
-
         w_raw = keep.tile([P, E * PASSES, PACK, N], F32, name="w_raw")
-        for e in range(E):
-            for g in range(PASSES):
-                nc.sync.dma_start(
-                    w_raw[:, e * PASSES + g, :, :],
-                    w[e, g * K_PASS : (g + 1) * K_PASS, :].rearrange("(p j) n -> p j n", j=PACK),
-                )
+        for kind, a in LOADS:
+            if kind == "p":
+                nc.sync.dma_start(planes[a][:], x_view[0, :, a, :])
+            elif kind == "r":
+                nc.sync.dma_start(raw1[:, a, :], x_view[1, :, a, :])
+            else:
+                for g in range(PASSES):
+                    nc.sync.dma_start(
+                        w_raw[:, a * PASSES + g, :, :],
+                        w[a, g * K_PASS : (g + 1) * K_PASS, :].rearrange("(p j) n -> p j n", j=PACK),
+                    )
 
         pos1_t = lists.tile([P, T // 16], U16, name="pos1_t")
         nc.sync.dma_start(pos1_t[:], pos1)
@@ -81,7 +76,7 @@ def tile_routed_moe_kernel(tc, xT, w, gate, offs, pos1, pos2, out):
                 nc.sync.dma_start(gt[:], gate[r, m * P : (m + 1) * P, :])
                 gate_t[(r, m)] = gt
 
-        xbf = keep.tile([P, PACK, T], BF16, name="xbf")
+        xbf = keep.tile([P, PACK, T], BF16, name="xbf", tag="xbf", align_bytes=64)
         for t in range(PACK):
             nc.scalar.copy(xbf[:, t, :], raw1[:, t, :])
 
@@ -95,36 +90,39 @@ def tile_routed_moe_kernel(tc, xT, w, gate, offs, pos1, pos2, out):
         g4s = {}
         for e in range(E):
             my_offs = offs_t[:, e * cols : (e + 1) * cols]
-            if V_FORM == "b":
-                for t in range(PACK):
-                    nc.vector.tensor_copy(xb[e][:, 0, :, t], raw0[:, t, :].indirect(my_offs))
-            else:
-                g4 = keep.tile([P, PACK, C], F32, name="g4_%d" % e)
-                for t in range(PACK):
-                    nc.vector.tensor_copy(g4[:, t, :], planes[t][:].indirect(my_offs))
-                g4s[e] = g4
+            g4 = keep.tile([P, PACK, C], F32, name="g4_%d" % e)
+            for t in range(PACK):
+                nc.vector.tensor_copy(g4[:, t, :], planes[t][:].indirect(my_offs))
+            g4s[e] = g4
             for t in range(PACK):
                 nc.scalar.activation(xb[e][:, 1, :, t], xbf[:, t, :].indirect(my_offs), COPY)
-        if V_FORM == "a":
-            for e in range(E):
-                move(X_ENG[e], xb[e][:, 0, :, :], g4s[e][:].rearrange("p t c -> p c t"))
+        for e in range(E):
+            move(X_ENG[e], xb[e][:, 0, :, :], g4s[e][:].rearrange("p t c -> p c t"))
 
         wbs, wcs, wss = {}, {}, {}
 
         def lay(i):
-            m, e0, ne, eng, tag = W_GROUPS[i]
+            m, e0, ne, tag, engs = W_GROUPS[i]
             u = ne * PASSES
             wbs[i] = keep.tile([P, u, P, PACK], BF16, name="wb%d" % i, tag=tag, align_bytes=64)
-            move(
-                eng,
-                wbs[i][:],
-                w_raw[:, e0 * PASSES : e0 * PASSES + u, :, m * P : (m + 1) * P].rearrange("p u j n -> p u n j"),
-            )
+            a = 0
+            while a < ne:
+                b = a + 1
+                while b < ne and engs[b] == engs[a]:
+                    b += 1
+                move(
+                    engs[a],
+                    wbs[i][:, a * PASSES : b * PASSES, :, :],
+                    w_raw[:, (e0 + a) * PASSES : (e0 + b) * PASSES, :, m * P : (m + 1) * P].rearrange(
+                        "p u j n -> p u n j"
+                    ),
+                )
+                a = b
 
         def quant_w(i):
-            m, e0, ne, eng, tag = W_GROUPS[i]
+            m, e0, ne, tag, engs = W_GROUPS[i]
             u = ne * PASSES
-            wcs[i] = keep.tile([P, u, P], U32, name="wc%d" % i, align_bytes=64)
+            wcs[i] = keep.tile([P, u, P], U32, name="wc%d" % i, tag=WC_TAGS[i], align_bytes=64)
             wss[i] = keep.tile([P, u, P], U8, name="ws%d" % i, align_bytes=64)
             nc.vector.quantize_mx(
                 out=wcs[i][:].rearrange("p u n -> p (u n)").bitcast(FP8X4),
@@ -136,7 +134,6 @@ def tile_routed_moe_kernel(tc, xT, w, gate, offs, pos1, pos2, out):
         lay(1)
         quant_w(0)
         quant_w(1)
-        XC_TAGS = ["wa","wbb","stage0","stage1"]
         for e in range(E):
             xc[e] = keep.tile([P, PASSES, C], U32, name="xc%d" % e, tag=XC_TAGS[e], align_bytes=64)
             nc.vector.quantize_mx(
@@ -149,7 +146,7 @@ def tile_routed_moe_kernel(tc, xT, w, gate, offs, pos1, pos2, out):
         quant_w(2)
         quant_w(3)
 
-        for i, (m, e0, ne, eng, tag) in enumerate(W_GROUPS):
+        for i, (m, e0, ne, tag, engs) in enumerate(W_GROUPS):
             wc, ws = wcs[i], wss[i]
             for e in range(e0, e0 + ne):
                 acc = psum.tile([P, C], F32, name="acc%d_%d" % (e, m))

@@ -20,24 +20,24 @@ PACK = 4
 K_PASS = P * PACK
 PASSES = K // K_PASS
 BLOCKS = N // P
+PAIR = 2
+PAIRS = E // PAIR
+WINDOW = 1024
 
-X_ENG = ["V","V","V","V"]
-W_GROUPS = [[0,0,2,"wa",["V","V"]],[0,2,2,"wbb",["V","V"]],[1,0,2,"stage2",["V","V"]],[1,2,2,"xbf",["S","S"]]]
-WC_TAGS = ["wc0","wc1","wc2","stage3"]
-XC_TAGS = ["wa","wbb","stage0","stage1"]
-Y_ENG = ["S","S","S","S","S","S","S","S"]
-LOADS = [["p",0],["r",0],["p",1],["r",1],["p",2],["r",2],["p",3],["r",3],["w",0],["w",1],["w",2],["w",3]]
+FAST_I = True
+FAST_W = True
+W_GROUPS = [[0,0,"wa","V","wc0"],[0,2,"wbb","V","wc1"],[1,0,"stage0","V","wc2"],[1,2,"xbf","S","stage1"]]
+XC_TAGS = ["wa","wbb"]
 
 
 def tile_routed_moe_kernel(tc, xT, w, gate, offs, pos1, pos2, out):
     nc = tc.nc
-    engines = {"S": nc.scalar, "V": nc.vector, "G": nc.gpsimd}
 
     def move(eng, dst, src):
         if eng == "S":
             nc.scalar.copy(dst, src)
         else:
-            engines[eng].tensor_copy(dst, src)
+            nc.vector.tensor_copy(dst, src)
 
     with ExitStack() as ctx:
         lists = ctx.enter_context(tc.tile_pool(name="lists", bufs=1))
@@ -48,20 +48,18 @@ def tile_routed_moe_kernel(tc, xT, w, gate, offs, pos1, pos2, out):
         nc.sync.dma_start(offs_t[:], offs)
 
         x_view = xT.rearrange("(g p t) n -> g p t n", p=P, t=PACK)
-        planes = [keep.tile([P, T], F32, name="plane%d" % t) for t in range(PACK)]
+        planes = [keep.tile([P, WINDOW], F32, name="plane%d" % t) for t in range(PACK)]
         raw1 = keep.tile([P, PACK, T], F32, name="raw1")
         w_raw = keep.tile([P, E * PASSES, PACK, N], F32, name="w_raw")
-        for kind, a in LOADS:
-            if kind == "p":
-                nc.sync.dma_start(planes[a][:], x_view[0, :, a, :])
-            elif kind == "r":
-                nc.sync.dma_start(raw1[:, a, :], x_view[1, :, a, :])
-            else:
-                for g in range(PASSES):
-                    nc.sync.dma_start(
-                        w_raw[:, a * PASSES + g, :, :],
-                        w[a, g * K_PASS : (g + 1) * K_PASS, :].rearrange("(p j) n -> p j n", j=PACK),
-                    )
+        for t in range(PACK):
+            nc.sync.dma_start(planes[t][:, 0:T], x_view[0, :, t, :])
+            nc.sync.dma_start(raw1[:, t, :], x_view[1, :, t, :])
+        for e in range(E):
+            for g in range(PASSES):
+                nc.sync.dma_start(
+                    w_raw[:, e * PASSES + g, :, :],
+                    w[e, g * K_PASS : (g + 1) * K_PASS, :].rearrange("(p j) n -> p j n", j=PACK),
+                )
 
         pos1_t = lists.tile([P, T // 16], U16, name="pos1_t")
         nc.sync.dma_start(pos1_t[:], pos1)
@@ -83,46 +81,55 @@ def tile_routed_moe_kernel(tc, xT, w, gate, offs, pos1, pos2, out):
         y_sb = [keep.tile([P, E * C], F32, name="y_sb%d" % m) for m in range(BLOCKS)]
 
         cols = C // 16
-        xb = [keep.tile([P, PASSES, C, PACK], BF16, name="xb%d" % e, tag="stage%d" % e, align_bytes=64) for e in range(E)]
+        xb = [
+            keep.tile([P, PASSES, PAIR * C, PACK], BF16, name="xb%d" % q, tag="stage%d" % q, align_bytes=64)
+            for q in range(PAIRS)
+        ]
         xc = {}
-        xs = [keep.tile([P, PASSES, C], U8, name="xs%d" % e, align_bytes=64) for e in range(E)]
+        xs = [keep.tile([P, PASSES, PAIR * C], U8, name="xs%d" % q, align_bytes=64) for q in range(PAIRS)]
 
         g4s = {}
-        for e in range(E):
-            my_offs = offs_t[:, e * cols : (e + 1) * cols]
-            g4 = keep.tile([P, PACK, C], F32, name="g4_%d" % e)
+        for q in range(PAIRS):
+            g4 = keep.tile([P, PACK, PAIR * C], F32, name="g4_%d" % q)
             for t in range(PACK):
-                nc.vector.tensor_copy(g4[:, t, :], planes[t][:].indirect(my_offs))
-            g4s[e] = g4
-            for t in range(PACK):
-                nc.scalar.activation(xb[e][:, 1, :, t], xbf[:, t, :].indirect(my_offs), COPY)
-        for e in range(E):
-            move(X_ENG[e], xb[e][:, 0, :, :], g4s[e][:].rearrange("p t c -> p c t"))
+                nc.vector.tensor_copy(
+                    g4[:, t, :], planes[t][:].indirect(offs_t[:, q * PAIR * cols : (q + 1) * PAIR * cols])
+                )
+            g4s[q] = g4
+            for e in range(q * PAIR, (q + 1) * PAIR):
+                a = (e - q * PAIR) * C
+                for t in range(PACK):
+                    nc.scalar.activation(
+                        xb[q][:, 1, a : a + C, t], xbf[:, t, :].indirect(offs_t[:, e * cols : (e + 1) * cols]), COPY
+                    )
+        for q in range(PAIRS):
+            if FAST_I:
+                nc.vector.tensor_copy(
+                    xb[q][:, 0, :, :].rearrange("p (c i) t -> p c t i", i=4),
+                    g4s[q][:].rearrange("p t (c i) -> p c t i", i=4),
+                )
+            else:
+                nc.vector.tensor_copy(xb[q][:, 0, :, :], g4s[q][:].rearrange("p t c -> p c t"))
 
         wbs, wcs, wss = {}, {}, {}
+        u = PAIR * PASSES
 
         def lay(i):
-            m, e0, ne, tag, engs = W_GROUPS[i]
-            u = ne * PASSES
+            m, e0, tag, eng, ctag = W_GROUPS[i]
             wbs[i] = keep.tile([P, u, P, PACK], BF16, name="wb%d" % i, tag=tag, align_bytes=64)
-            a = 0
-            while a < ne:
-                b = a + 1
-                while b < ne and engs[b] == engs[a]:
-                    b += 1
+            src = w_raw[:, e0 * PASSES : e0 * PASSES + u, :, m * P : (m + 1) * P]
+            if FAST_W:
                 move(
-                    engs[a],
-                    wbs[i][:, a * PASSES : b * PASSES, :, :],
-                    w_raw[:, (e0 + a) * PASSES : (e0 + b) * PASSES, :, m * P : (m + 1) * P].rearrange(
-                        "p u j n -> p u n j"
-                    ),
+                    eng,
+                    wbs[i][:].rearrange("p u (c i) j -> p u c j i", i=4),
+                    src.rearrange("p u j (c i) -> p u c j i", i=4),
                 )
-                a = b
+            else:
+                move(eng, wbs[i][:], src.rearrange("p u j n -> p u n j"))
 
         def quant_w(i):
-            m, e0, ne, tag, engs = W_GROUPS[i]
-            u = ne * PASSES
-            wcs[i] = keep.tile([P, u, P], U32, name="wc%d" % i, tag=WC_TAGS[i], align_bytes=64)
+            m, e0, tag, eng, ctag = W_GROUPS[i]
+            wcs[i] = keep.tile([P, u, P], U32, name="wc%d" % i, tag=ctag, align_bytes=64)
             wss[i] = keep.tile([P, u, P], U8, name="ws%d" % i, align_bytes=64)
             nc.vector.quantize_mx(
                 out=wcs[i][:].rearrange("p u n -> p (u n)").bitcast(FP8X4),
@@ -134,33 +141,34 @@ def tile_routed_moe_kernel(tc, xT, w, gate, offs, pos1, pos2, out):
         lay(1)
         quant_w(0)
         quant_w(1)
-        for e in range(E):
-            xc[e] = keep.tile([P, PASSES, C], U32, name="xc%d" % e, tag=XC_TAGS[e], align_bytes=64)
+        for q in range(PAIRS):
+            xc[q] = keep.tile([P, PASSES, PAIR * C], U32, name="xc%d" % q, tag=XC_TAGS[q], align_bytes=64)
             nc.vector.quantize_mx(
-                out=xc[e][:].rearrange("p g c -> p (g c)").bitcast(FP8X4),
-                scales=xs[e][:].rearrange("p g c -> p (g c)"),
-                in_=xb[e][:].rearrange("p g c t -> p (g c t)"),
+                out=xc[q][:].rearrange("p g c -> p (g c)").bitcast(FP8X4),
+                scales=xs[q][:].rearrange("p g c -> p (g c)"),
+                in_=xb[q][:].rearrange("p g c t -> p (g c t)"),
             )
         lay(2)
         lay(3)
         quant_w(2)
         quant_w(3)
 
-        for i, (m, e0, ne, tag, engs) in enumerate(W_GROUPS):
+        for i, (m, e0, tag, eng, ctag) in enumerate(W_GROUPS):
             wc, ws = wcs[i], wss[i]
-            for e in range(e0, e0 + ne):
+            for e in range(e0, e0 + PAIR):
+                q, a = e // PAIR, (e % PAIR) * C
                 acc = psum.tile([P, C], F32, name="acc%d_%d" % (e, m))
                 for g in range(PASSES):
                     nc.tensor.matmul_mx(
                         out=acc[:],
                         lhsT=wc[:, (e - e0) * PASSES + g, :].bitcast(FP8X4),
                         lhsT_scale=ws[:, (e - e0) * PASSES + g, :],
-                        rhs=xc[e][:, g, :].bitcast(FP8X4),
-                        rhs_scale=xs[e][:, g, :],
+                        rhs=xc[q][:, g, a : a + C].bitcast(FP8X4),
+                        rhs_scale=xs[q][:, g, a : a + C],
                         start=(g == 0),
                         stop=(g == PASSES - 1),
                     )
-                move(Y_ENG[m * E + e], y_sb[m][:, e * C : (e + 1) * C], acc[:])
+                nc.scalar.copy(y_sb[m][:, e * C : (e + 1) * C], acc[:])
 
         for m in range(BLOCKS):
             parts = []

@@ -24,10 +24,11 @@ PAIR = 2
 PAIRS = E // PAIR
 WINDOW = 1024
 
-FAST_I = True
-FAST_W = True
-W_GROUPS = [[0,0,"wa","V","wc0"],[0,2,"wbb","V","wc1"],[1,0,"stage0","V","wc2"],[1,2,"xbf","S","stage1"]]
-XC_TAGS = ["wa","wbb"]
+LOADS = [("p", 0), ("r", 0), ("p", 1), ("r", 1), ("w", 0, 0), ("w", 0, 1), ("p", 2), ("r", 2), ("p", 3), ("r", 3), ("w", 1, 0), ("w", 1, 1), ("w", 2, 0), ("w", 2, 1), ("w", 3, 0), ("w", 3, 1)]
+CASTS = "SSSS"
+W_GROUPS = [(0, 0, "wa", "GV", "wc0"), (0, 2, "wbb", "V", "wc1"), (1, 0, "wg2", "GV", "wc2"), (1, 2, "xbf", "S", "stage1")]
+XC_TAGS = ["wa", "wbb"]
+W_TEXT = [("lay", 0), ("lay", 1), ("quant", 0), ("quant", 1), ("tq", 0), ("tq", 1), ("lay", 2), ("lay", 3), ("quant", 2), ("quant", 3)]
 
 
 def tile_routed_moe_kernel(tc, xT, w, gate, offs, pos1, pos2, out):
@@ -36,6 +37,8 @@ def tile_routed_moe_kernel(tc, xT, w, gate, offs, pos1, pos2, out):
     def move(eng, dst, src):
         if eng == "S":
             nc.scalar.copy(dst, src)
+        elif eng == "G":
+            nc.gpsimd.tensor_copy(dst, src)
         else:
             nc.vector.tensor_copy(dst, src)
 
@@ -51,11 +54,13 @@ def tile_routed_moe_kernel(tc, xT, w, gate, offs, pos1, pos2, out):
         planes = [keep.tile([P, WINDOW], F32, name="plane%d" % t) for t in range(PACK)]
         raw1 = keep.tile([P, PACK, T], F32, name="raw1")
         w_raw = keep.tile([P, E * PASSES, PACK, N], F32, name="w_raw")
-        for t in range(PACK):
-            nc.sync.dma_start(planes[t][:, 0:T], x_view[0, :, t, :])
-            nc.sync.dma_start(raw1[:, t, :], x_view[1, :, t, :])
-        for e in range(E):
-            for g in range(PASSES):
+        for item in LOADS:
+            if item[0] == "p":
+                nc.sync.dma_start(planes[item[1]][:, 0:T], x_view[0, :, item[1], :])
+            elif item[0] == "r":
+                nc.sync.dma_start(raw1[:, item[1], :], x_view[1, :, item[1], :])
+            else:
+                e, g = item[1], item[2]
                 nc.sync.dma_start(
                     w_raw[:, e * PASSES + g, :, :],
                     w[e, g * K_PASS : (g + 1) * K_PASS, :].rearrange("(p j) n -> p j n", j=PACK),
@@ -76,7 +81,7 @@ def tile_routed_moe_kernel(tc, xT, w, gate, offs, pos1, pos2, out):
 
         xbf = keep.tile([P, PACK, T], BF16, name="xbf", tag="xbf", align_bytes=64)
         for t in range(PACK):
-            nc.scalar.copy(xbf[:, t, :], raw1[:, t, :])
+            move(CASTS[t], xbf[:, t, :], raw1[:, t, :])
 
         y_sb = [keep.tile([P, E * C], F32, name="y_sb%d" % m) for m in range(BLOCKS)]
 
@@ -103,32 +108,33 @@ def tile_routed_moe_kernel(tc, xT, w, gate, offs, pos1, pos2, out):
                         xb[q][:, 1, a : a + C, t], xbf[:, t, :].indirect(offs_t[:, e * cols : (e + 1) * cols]), COPY
                     )
         for q in range(PAIRS):
-            if FAST_I:
-                nc.vector.tensor_copy(
-                    xb[q][:, 0, :, :].rearrange("p (c i) t -> p c t i", i=4),
-                    g4s[q][:].rearrange("p t (c i) -> p c t i", i=4),
-                )
-            else:
-                nc.vector.tensor_copy(xb[q][:, 0, :, :], g4s[q][:].rearrange("p t c -> p c t"))
+            nc.vector.tensor_copy(
+                xb[q][:, 0, :, :].rearrange("p (c i) t -> p c t i", i=4),
+                g4s[q][:].rearrange("p t (c i) -> p c t i", i=4),
+            )
 
         wbs, wcs, wss = {}, {}, {}
         u = PAIR * PASSES
 
         def lay(i):
-            m, e0, tag, eng, ctag = W_GROUPS[i]
+            m, e0, tag, engs, ctag = W_GROUPS[i]
             wbs[i] = keep.tile([P, u, P, PACK], BF16, name="wb%d" % i, tag=tag, align_bytes=64)
-            src = w_raw[:, e0 * PASSES : e0 * PASSES + u, :, m * P : (m + 1) * P]
-            if FAST_W:
-                move(
-                    eng,
-                    wbs[i][:].rearrange("p u (c i) j -> p u c j i", i=4),
-                    src.rearrange("p u j (c i) -> p u c j i", i=4),
-                )
-            else:
-                move(eng, wbs[i][:], src.rearrange("p u j n -> p u n j"))
+            n_cut = len(engs)
+            step = u // n_cut
+            for k in range(n_cut):
+                src = w_raw[:, e0 * PASSES + k * step : e0 * PASSES + (k + 1) * step, :, m * P : (m + 1) * P]
+                dst = wbs[i][:, k * step : (k + 1) * step, :, :]
+                if engs[k] == "G":
+                    move(engs[k], dst, src.rearrange("p u j n -> p u n j"))
+                else:
+                    move(
+                        engs[k],
+                        dst.rearrange("p u (c i) j -> p u c j i", i=4),
+                        src.rearrange("p u j (c i) -> p u c j i", i=4),
+                    )
 
         def quant_w(i):
-            m, e0, tag, eng, ctag = W_GROUPS[i]
+            m, e0, tag, engs, ctag = W_GROUPS[i]
             wcs[i] = keep.tile([P, u, P], U32, name="wc%d" % i, tag=ctag, align_bytes=64)
             wss[i] = keep.tile([P, u, P], U8, name="ws%d" % i, align_bytes=64)
             nc.vector.quantize_mx(
@@ -137,23 +143,23 @@ def tile_routed_moe_kernel(tc, xT, w, gate, offs, pos1, pos2, out):
                 in_=wbs[i][:].rearrange("p u n j -> p (u n j)"),
             )
 
-        lay(0)
-        lay(1)
-        quant_w(0)
-        quant_w(1)
-        for q in range(PAIRS):
+        def quant_x(q):
             xc[q] = keep.tile([P, PASSES, PAIR * C], U32, name="xc%d" % q, tag=XC_TAGS[q], align_bytes=64)
             nc.vector.quantize_mx(
                 out=xc[q][:].rearrange("p g c -> p (g c)").bitcast(FP8X4),
                 scales=xs[q][:].rearrange("p g c -> p (g c)"),
                 in_=xb[q][:].rearrange("p g c t -> p (g c t)"),
             )
-        lay(2)
-        lay(3)
-        quant_w(2)
-        quant_w(3)
 
-        for i, (m, e0, tag, eng, ctag) in enumerate(W_GROUPS):
+        for what, i in W_TEXT:
+            if what == "lay":
+                lay(i)
+            elif what == "quant":
+                quant_w(i)
+            else:
+                quant_x(i)
+
+        for i, (m, e0, tag, engs, ctag) in enumerate(W_GROUPS):
             wc, ws = wcs[i], wss[i]
             for e in range(e0, e0 + PAIR):
                 q, a = e // PAIR, (e % PAIR) * C

@@ -24,11 +24,11 @@ PAIR = 2
 PAIRS = E // PAIR
 WINDOW = 1024
 
-LOADS = [("p", 0), ("r", 0), ("p", 1), ("r", 1), ("w", 0, 0), ("w", 0, 1), ("p", 2), ("r", 2), ("p", 3), ("r", 3), ("w", 1, 0), ("w", 1, 1), ("w", 2, 0), ("w", 2, 1), ("w", 3, 0), ("w", 3, 1)]
-CASTS = "SSSS"
-W_GROUPS = [(0, 0, "wa", "GV", "wc0"), (0, 2, "wbb", "V", "wc1"), (1, 0, "wg2", "GV", "wc2"), (1, 2, "xbf", "S", "stage1")]
+LOADS = [("p", 0), ("r", 0), ("p", 1), ("r", 1), ("r", 2), ("r", 3), ("p", 2), ("w", 0, 0), ("w", 0, 1), ("p", 3), ("w", 1, 0), ("w", 1, 1), ("w", 2, 0), ("w", 2, 1), ("w", 3, 0), ("w", 3, 1)]
+CASTS = "SGGG"
+W_GROUPS = [(0, 0, 2, "wa", "GV", "wc0"), (0, 2, 2, "wbb", "V", "wc1"), (1, 0, 1, "wg2", "G", "xbf"), (1, 1, 1, "stage1", "V", "wc3"), (1, 2, 2, "xbf", "S", "stage1")]
 XC_TAGS = ["wa", "wbb"]
-W_TEXT = [("lay", 0), ("lay", 1), ("quant", 0), ("quant", 1), ("tq", 0), ("tq", 1), ("lay", 2), ("lay", 3), ("quant", 2), ("quant", 3)]
+W_TEXT = [("lay", 0), ("lay", 2), ("lay", 1), ("quant", 0), ("quant", 1), ("tq", 0), ("tq", 1), ("lay", 3), ("lay", 4), ("quant", 3), ("quant", 4), ("quant", 2)]
 
 
 def tile_routed_moe_kernel(tc, xT, w, gate, offs, pos1, pos2, out):
@@ -114,10 +114,10 @@ def tile_routed_moe_kernel(tc, xT, w, gate, offs, pos1, pos2, out):
             )
 
         wbs, wcs, wss = {}, {}, {}
-        u = PAIR * PASSES
 
         def lay(i):
-            m, e0, tag, engs, ctag = W_GROUPS[i]
+            m, e0, ne, tag, engs, ctag = W_GROUPS[i]
+            u = ne * PASSES
             wbs[i] = keep.tile([P, u, P, PACK], BF16, name="wb%d" % i, tag=tag, align_bytes=64)
             n_cut = len(engs)
             step = u // n_cut
@@ -134,7 +134,8 @@ def tile_routed_moe_kernel(tc, xT, w, gate, offs, pos1, pos2, out):
                     )
 
         def quant_w(i):
-            m, e0, tag, engs, ctag = W_GROUPS[i]
+            m, e0, ne, tag, engs, ctag = W_GROUPS[i]
+            u = ne * PASSES
             wcs[i] = keep.tile([P, u, P], U32, name="wc%d" % i, tag=ctag, align_bytes=64)
             wss[i] = keep.tile([P, u, P], U8, name="ws%d" % i, align_bytes=64)
             nc.vector.quantize_mx(
@@ -159,9 +160,9 @@ def tile_routed_moe_kernel(tc, xT, w, gate, offs, pos1, pos2, out):
             else:
                 quant_x(i)
 
-        for i, (m, e0, tag, engs, ctag) in enumerate(W_GROUPS):
+        for i, (m, e0, ne, tag, engs, ctag) in enumerate(W_GROUPS):
             wc, ws = wcs[i], wss[i]
-            for e in range(e0, e0 + PAIR):
+            for e in range(e0, e0 + ne):
                 q, a = e // PAIR, (e % PAIR) * C
                 acc = psum.tile([P, C], F32, name="acc%d_%d" % (e, m))
                 for g in range(PASSES):

@@ -1,6 +1,7 @@
 from contextlib import ExitStack
 
 import concourse.mybir as mybir
+from concourse.masks import make_identity
 
 K, T, E, C, N = 1024, 512, 4, 256, 256
 FLOPS = 2 * K * N * E * C
@@ -24,11 +25,12 @@ PAIR = 2
 PAIRS = E // PAIR
 WINDOW = 1024
 
-LOADS = [("p", 0), ("r", 0), ("p", 1), ("r", 1), ("r", 2), ("r", 3), ("p", 2), ("w", 0, 0), ("w", 0, 1), ("p", 3), ("w", 1, 0), ("w", 1, 1), ("w", 2, 0), ("w", 2, 1), ("w", 3, 0), ("w", 3, 1)]
+LOADS = [("p", 0), ("r", 0), ("p", 1), ("r", 1), ("r", 2), ("r", 3), ("p", 2), ("w", 0), ("p", 3), ("w", 1), ("w", 2), ("w", 3)]
 CASTS = "SGGG"
-W_GROUPS = [(0, 0, 2, "wa", "GV", "wc0"), (0, 2, 2, "wbb", "V", "wc1"), (1, 0, 1, "wg2", "G", "xbf"), (1, 1, 1, "stage1", "V", "wc3"), (1, 2, 2, "xbf", "S", "stage1")]
-XC_TAGS = ["wa", "wbb"]
-W_TEXT = [("lay", 0), ("lay", 2), ("lay", 1), ("quant", 0), ("quant", 1), ("tq", 0), ("tq", 1), ("lay", 3), ("lay", 4), ("quant", 3), ("quant", 4), ("quant", 2)]
+W_GROUPS = [(0, 0, 4, "wab", [("G", 0, 1), ("V", 1, 1), ("V", 2, 2)], "wc0"), (1, 0, 1, "wg2", [("G", 0, 1)], "xbf"), (1, 1, 1, "stage", [("V", 0, 1)], "wc3"), (1, 2, 2, "xbf", [("S", 0, 2)], "stage")]
+XC_TAGS = ["xc0", "wab"]
+W_TEXT = [("lay", 0), ("lay", 1), ("tq", 0), ("quant", 0), ("tq", 1), ("lay", 2), ("lay", 3), ("quant", 2), ("quant", 3), ("quant", 1)]
+PE_ADD = False
 
 
 def tile_routed_moe_kernel(tc, xT, w, gate, offs, pos1, pos2, out):
@@ -50,6 +52,10 @@ def tile_routed_moe_kernel(tc, xT, w, gate, offs, pos1, pos2, out):
         offs_t = lists.tile([P, E * C // 16], U16, name="offs_t")
         nc.sync.dma_start(offs_t[:], offs)
 
+        ident = keep.tile([P, P], F32, name="ident")
+        if PE_ADD:
+            make_identity(nc, ident[:])
+
         x_view = xT.rearrange("(g p t) n -> g p t n", p=P, t=PACK)
         planes = [keep.tile([P, WINDOW], F32, name="plane%d" % t) for t in range(PACK)]
         raw1 = keep.tile([P, PACK, T], F32, name="raw1")
@@ -59,6 +65,12 @@ def tile_routed_moe_kernel(tc, xT, w, gate, offs, pos1, pos2, out):
                 nc.sync.dma_start(planes[item[1]][:, 0:T], x_view[0, :, item[1], :])
             elif item[0] == "r":
                 nc.sync.dma_start(raw1[:, item[1], :], x_view[1, :, item[1], :])
+            elif len(item) == 2:
+                e = item[1]
+                nc.sync.dma_start(
+                    w_raw[:, e * PASSES : (e + 1) * PASSES, :, :].rearrange("p g j n -> p g (j n)"),
+                    w[e].rearrange("(g p j) n -> p g (j n)", p=P, j=PACK),
+                )
             else:
                 e, g = item[1], item[2]
                 nc.sync.dma_start(
@@ -86,70 +98,61 @@ def tile_routed_moe_kernel(tc, xT, w, gate, offs, pos1, pos2, out):
         y_sb = [keep.tile([P, E * C], F32, name="y_sb%d" % m) for m in range(BLOCKS)]
 
         cols = C // 16
-        xb = [
-            keep.tile([P, PASSES, PAIR * C, PACK], BF16, name="xb%d" % q, tag="stage%d" % q, align_bytes=64)
-            for q in range(PAIRS)
-        ]
-        xc = {}
-        xs = [keep.tile([P, PASSES, PAIR * C], U8, name="xs%d" % q, align_bytes=64) for q in range(PAIRS)]
-
-        g4s = {}
+        xb = keep.tile([P, PAIRS, PASSES, PAIR * C, PACK], BF16, name="xb", tag="stage", align_bytes=64)
+        xs = keep.tile([P, PAIRS, PASSES, PAIR * C], U8, name="xs", align_bytes=64)
+        g4 = keep.tile([P, PACK, E * C], F32, name="g4")
         for q in range(PAIRS):
-            g4 = keep.tile([P, PACK, PAIR * C], F32, name="g4_%d" % q)
             for t in range(PACK):
                 nc.vector.tensor_copy(
-                    g4[:, t, :], planes[t][:].indirect(offs_t[:, q * PAIR * cols : (q + 1) * PAIR * cols])
+                    g4[:, t, q * PAIR * C : (q + 1) * PAIR * C],
+                    planes[t][:].indirect(offs_t[:, q * PAIR * cols : (q + 1) * PAIR * cols]),
                 )
-            g4s[q] = g4
             for e in range(q * PAIR, (q + 1) * PAIR):
                 a = (e - q * PAIR) * C
                 for t in range(PACK):
                     nc.scalar.activation(
-                        xb[q][:, 1, a : a + C, t], xbf[:, t, :].indirect(offs_t[:, e * cols : (e + 1) * cols]), COPY
+                        xb[:, q, 1, a : a + C, t], xbf[:, t, :].indirect(offs_t[:, e * cols : (e + 1) * cols]), COPY
                     )
-        for q in range(PAIRS):
-            nc.vector.tensor_copy(
-                xb[q][:, 0, :, :].rearrange("p (c i) t -> p c t i", i=4),
-                g4s[q][:].rearrange("p t (c i) -> p c t i", i=4),
-            )
+        nc.vector.tensor_copy(
+            xb[:, :, 0, :, :].rearrange("p q (c i) t -> p q c t i", i=4),
+            g4[:].rearrange("p t (q c i) -> p q c t i", q=PAIRS, i=4),
+        )
 
         wbs, wcs, wss = {}, {}, {}
 
         def lay(i):
-            m, e0, ne, tag, engs, ctag = W_GROUPS[i]
-            u = ne * PASSES
-            wbs[i] = keep.tile([P, u, P, PACK], BF16, name="wb%d" % i, tag=tag, align_bytes=64)
-            n_cut = len(engs)
-            step = u // n_cut
-            for k in range(n_cut):
-                src = w_raw[:, e0 * PASSES + k * step : e0 * PASSES + (k + 1) * step, :, m * P : (m + 1) * P]
-                dst = wbs[i][:, k * step : (k + 1) * step, :, :]
-                if engs[k] == "G":
-                    move(engs[k], dst, src.rearrange("p u j n -> p u n j"))
+            m, e0, ne, tag, cuts, ctag = W_GROUPS[i]
+            wbs[i] = keep.tile([P, ne * PASSES, P, PACK], BF16, name="wb%d" % i, tag=tag, align_bytes=64)
+            for eng, k0, kn in cuts:
+                src = w_raw[:, (e0 + k0) * PASSES : (e0 + k0 + kn) * PASSES, :, m * P : (m + 1) * P]
+                dst = wbs[i][:, k0 * PASSES : (k0 + kn) * PASSES, :, :]
+                if eng == "G":
+                    move(eng, dst, src.rearrange("p u j n -> p u n j"))
                 else:
                     move(
-                        engs[k],
+                        eng,
                         dst.rearrange("p u (c i) j -> p u c j i", i=4),
                         src.rearrange("p u j (c i) -> p u c j i", i=4),
                     )
 
         def quant_w(i):
-            m, e0, ne, tag, engs, ctag = W_GROUPS[i]
-            u = ne * PASSES
-            wcs[i] = keep.tile([P, u, P], U32, name="wc%d" % i, tag=ctag, align_bytes=64)
-            wss[i] = keep.tile([P, u, P], U8, name="ws%d" % i, align_bytes=64)
+            m, e0, ne, tag, cuts, ctag = W_GROUPS[i]
+            wcs[i] = keep.tile([P, ne * PASSES, P], U32, name="wc%d" % i, tag=ctag, align_bytes=64)
+            wss[i] = keep.tile([P, ne * PASSES, P], U8, name="ws%d" % i, align_bytes=64)
             nc.vector.quantize_mx(
                 out=wcs[i][:].rearrange("p u n -> p (u n)").bitcast(FP8X4),
                 scales=wss[i][:].rearrange("p u n -> p (u n)"),
                 in_=wbs[i][:].rearrange("p u n j -> p (u n j)"),
             )
 
+        xc = {}
+
         def quant_x(q):
             xc[q] = keep.tile([P, PASSES, PAIR * C], U32, name="xc%d" % q, tag=XC_TAGS[q], align_bytes=64)
             nc.vector.quantize_mx(
                 out=xc[q][:].rearrange("p g c -> p (g c)").bitcast(FP8X4),
-                scales=xs[q][:].rearrange("p g c -> p (g c)"),
-                in_=xb[q][:].rearrange("p g c t -> p (g c t)"),
+                scales=xs[:, q, :, :].rearrange("p g c -> p (g c)"),
+                in_=xb[:, q, :, :, :].rearrange("p g c t -> p (g c t)"),
             )
 
         for what, i in W_TEXT:
@@ -160,7 +163,7 @@ def tile_routed_moe_kernel(tc, xT, w, gate, offs, pos1, pos2, out):
             else:
                 quant_x(i)
 
-        for i, (m, e0, ne, tag, engs, ctag) in enumerate(W_GROUPS):
+        for i, (m, e0, ne, tag, cuts, ctag) in enumerate(W_GROUPS):
             wc, ws = wcs[i], wss[i]
             for e in range(e0, e0 + ne):
                 q, a = e // PAIR, (e % PAIR) * C
@@ -171,7 +174,7 @@ def tile_routed_moe_kernel(tc, xT, w, gate, offs, pos1, pos2, out):
                         lhsT=wc[:, (e - e0) * PASSES + g, :].bitcast(FP8X4),
                         lhsT_scale=ws[:, (e - e0) * PASSES + g, :],
                         rhs=xc[q][:, g, a : a + C].bitcast(FP8X4),
-                        rhs_scale=xs[q][:, g, a : a + C],
+                        rhs_scale=xs[:, q, g, a : a + C],
                         start=(g == 0),
                         stop=(g == PASSES - 1),
                     )
@@ -184,5 +187,11 @@ def tile_routed_moe_kernel(tc, xT, w, gate, offs, pos1, pos2, out):
                 nc.vector.tensor_tensor(part[:], y_sb[m][:].indirect(pos_t[r][:]), gate_t[(r, m)][:], MULT)
                 parts.append(part)
             res = keep.tile([P, T], F32, name="res%d" % m)
-            nc.vector.tensor_tensor(res[:], parts[0][:], parts[1][:], ADD)
+            if PE_ADD and m == 0:
+                total = psum.tile([P, T], F32, name="total", tag="acc%d_%d" % (E - 1, BLOCKS - 1))
+                nc.tensor.matmul(total[:], lhsT=ident[:], rhs=parts[0][:], start=True, stop=False)
+                nc.tensor.matmul(total[:], lhsT=ident[:], rhs=parts[1][:], start=False, stop=True)
+                nc.scalar.copy(res[:], total[:])
+            else:
+                nc.vector.tensor_tensor(res[:], parts[0][:], parts[1][:], ADD)
             nc.sync.dma_start(out[m * P : (m + 1) * P, :], res[:])

@@ -31,6 +31,9 @@ W_GROUPS = [(0, 0, 4, "wab", [("G", 0, 1), ("V", 1, 1), ("V", 2, 2)], "wc0"), (1
 XC_TAGS = ["xc0", "wab"]
 W_TEXT = [("lay", 0), ("lay", 1), ("tq", 0), ("quant", 0), ("tq", 1), ("lay", 2), ("lay", 3), ("quant", 2), ("quant", 3), ("quant", 1)]
 PE_ADD = False
+RES_TAGS = ["gate0_1", "res1"]
+TI_SPLIT = True
+TAIL_CUT = False
 
 
 def tile_routed_moe_kernel(tc, xT, w, gate, offs, pos1, pos2, out):
@@ -113,10 +116,17 @@ def tile_routed_moe_kernel(tc, xT, w, gate, offs, pos1, pos2, out):
                     nc.scalar.activation(
                         xb[:, q, 1, a : a + C, t], xbf[:, t, :].indirect(offs_t[:, e * cols : (e + 1) * cols]), COPY
                     )
-        nc.vector.tensor_copy(
-            xb[:, :, 0, :, :].rearrange("p q (c i) t -> p q c t i", i=4),
-            g4[:].rearrange("p t (q c i) -> p q c t i", q=PAIRS, i=4),
-        )
+        if TI_SPLIT:
+            for q in range(PAIRS):
+                nc.vector.tensor_copy(
+                    xb[:, q, 0, :, :].rearrange("p (c i) t -> p c t i", i=4),
+                    g4[:, :, q * PAIR * C : (q + 1) * PAIR * C].rearrange("p t (c i) -> p c t i", i=4),
+                )
+        else:
+            nc.vector.tensor_copy(
+                xb[:, :, 0, :, :].rearrange("p q (c i) t -> p q c t i", i=4),
+                g4[:].rearrange("p t (q c i) -> p q c t i", q=PAIRS, i=4),
+            )
 
         wbs, wcs, wss = {}, {}, {}
 
@@ -182,11 +192,27 @@ def tile_routed_moe_kernel(tc, xT, w, gate, offs, pos1, pos2, out):
 
         for m in range(BLOCKS):
             parts = []
+            cut = TAIL_CUT and m == BLOCKS - 1
             for r in range(2):
                 part = keep.tile([P, T], F32, name="part%d_%d" % (r, m))
-                nc.vector.tensor_tensor(part[:], y_sb[m][:].indirect(pos_t[r][:]), gate_t[(r, m)][:], MULT)
+                if cut and r == 1:
+                    for h in range(2):
+                        nc.vector.tensor_tensor(
+                            part[:, h * (T // 2) : (h + 1) * (T // 2)],
+                            y_sb[m][:].indirect(pos_t[r][:, h * (T // 32) : (h + 1) * (T // 32)]),
+                            gate_t[(r, m)][:, h * (T // 2) : (h + 1) * (T // 2)],
+                            MULT,
+                        )
+                else:
+                    nc.vector.tensor_tensor(part[:], y_sb[m][:].indirect(pos_t[r][:]), gate_t[(r, m)][:], MULT)
                 parts.append(part)
-            res = keep.tile([P, T], F32, name="res%d" % m)
+            res = keep.tile([P, T], F32, name="res%d" % m, tag=RES_TAGS[m])
+            if cut:
+                for h in range(2):
+                    hs = slice(h * (T // 2), (h + 1) * (T // 2))
+                    nc.vector.tensor_tensor(res[:, hs], parts[0][:, hs], parts[1][:, hs], ADD)
+                    nc.sync.dma_start(out[m * P : (m + 1) * P, hs], res[:, hs])
+                continue
             if PE_ADD and m == 0:
                 total = psum.tile([P, T], F32, name="total", tag="acc%d_%d" % (E - 1, BLOCKS - 1))
                 nc.tensor.matmul(total[:], lhsT=ident[:], rhs=parts[0][:], start=True, stop=False)

@@ -33,7 +33,7 @@ W_TEXT = [("lay", 0), ("lay", 1), ("tq", 0), ("quant", 0), ("tq", 1), ("lay", 2)
 PE_ADD = False
 RES_TAGS = ["gate0_1", "res1"]
 TI_SPLIT = True
-TAIL_CUT = False
+TAIL_CUT = True
 
 
 def tile_routed_moe_kernel(tc, xT, w, gate, offs, pos1, pos2, out):

@@ -27,9 +27,9 @@ WINDOW = 1024
 
 LOADS = [("p", 0), ("r", 0), ("p", 1), ("r", 1), ("r", 2), ("r", 3), ("p", 2), ("w", 0), ("p", 3), ("w", 1), ("w", 2), ("w", 3)]
 CASTS = "SGGG"
-W_GROUPS = [(0, 0, 4, "wab", [("G", 0, 1), ("V", 1, 1), ("V", 2, 2)], "wc0"), (1, 0, 1, "wg2", [("G", 0, 1)], "xbf"), (1, 1, 1, "stage", [("V", 0, 1)], "wc3"), (1, 2, 2, "xbf", [("S", 0, 2)], "stage")]
+W_GROUPS = [(0, 0, 4, "wab", [("G", 0, 1), ("V", 1, 1), ("V", 2, 2)], "wc0"), (1, 0, 1, "wg2", [("G", 0, 1)], "xbf"), (1, 1, 2, "xbf", [("S", 0, 2)], "stage"), (1, 3, 1, "wv3", [("V", 0, 1)], "wc3")]
 XC_TAGS = ["xc0", "wab"]
-W_TEXT = [("lay", 0), ("lay", 1), ("tq", 0), ("quant", 0), ("tq", 1), ("lay", 2), ("lay", 3), ("quant", 2), ("quant", 3), ("quant", 1)]
+W_TEXT = [("lay", 0), ("lay", 1), ("tq", 0), ("lay", 3), ("quant", 0), ("tq", 1), ("lay", 2), ("quant", 3), ("quant", 2), ("quant", 1)]
 PE_ADD = False
 RES_TAGS = ["gate0_1", "res1"]
 TI_SPLIT = True

@@ -104,6 +104,7 @@ def tile_routed_moe_kernel(tc, xT, w, gate, offs, pos1, pos2, out):
         xb = keep.tile([P, PAIRS, PASSES, PAIR * C, PACK], BF16, name="xb", tag="stage", align_bytes=64)
         xs = keep.tile([P, PAIRS, PASSES, PAIR * C], U8, name="xs", align_bytes=64)
         g4 = keep.tile([P, PACK, E * C], F32, name="g4")
+        xh = keep.tile([P, PAIRS, 2, PAIR * C, 2], BF16, name="xh", align_bytes=64)
         for q in range(PAIRS):
             for t in range(PACK):
                 nc.vector.tensor_copy(
@@ -114,8 +115,12 @@ def tile_routed_moe_kernel(tc, xT, w, gate, offs, pos1, pos2, out):
                 a = (e - q * PAIR) * C
                 for t in range(PACK):
                     nc.scalar.activation(
-                        xb[:, q, 1, a : a + C, t], xbf[:, t, :].indirect(offs_t[:, e * cols : (e + 1) * cols]), COPY
+                        xh[:, q, t // 2, a : a + C, t % 2], xbf[:, t, :].indirect(offs_t[:, e * cols : (e + 1) * cols]), COPY
                     )
+            nc.scalar.copy(
+                xb[:, q, 1, :, :].rearrange("p c t -> p (c t)").bitcast(F32).rearrange("p (c h) -> p c h", h=2),
+                xh[:, q, :, :, :].rearrange("p h c e -> p (h c e)").bitcast(F32).rearrange("p (h c) -> p c h", h=2),
+            )
         if TI_SPLIT:
             for q in range(PAIRS):
                 nc.vector.tensor_copy(

@@ -34,6 +34,7 @@ PE_ADD = False
 RES_TAGS = ["gate0_1", "res1"]
 TI_SPLIT = True
 TAIL_CUT = True
+BLOCK_OF = {(0, 1): 0, (0, 0): 1, (1, 0): 2, (1, 1): 3}
 
 
 def tile_routed_moe_kernel(tc, xT, w, gate, offs, pos1, pos2, out):
@@ -104,29 +105,40 @@ def tile_routed_moe_kernel(tc, xT, w, gate, offs, pos1, pos2, out):
         xb = keep.tile([P, PAIRS, PASSES, PAIR * C, PACK], BF16, name="xb", tag="stage", align_bytes=64)
         xs = keep.tile([P, PAIRS, PASSES, PAIR * C], U8, name="xs", align_bytes=64)
         g4 = keep.tile([P, PACK, E * C], F32, name="g4")
-        xh = keep.tile([P, PAIRS, 2, PAIR * C, 2], BF16, name="xh", align_bytes=64)
+        xbe = xb[:, 1, :, :, :].rearrange("p g c t -> p (g c t)").rearrange("p (b c t) -> p b c t", b=PAIR * PASSES, t=PACK)
         for q in range(PAIRS):
             for t in range(PACK):
                 nc.vector.tensor_copy(
                     g4[:, t, q * PAIR * C : (q + 1) * PAIR * C],
                     planes[t][:].indirect(offs_t[:, q * PAIR * cols : (q + 1) * PAIR * cols]),
                 )
+            xh = keep.tile([P, 2, PAIR * C, 2], BF16, name="xh%d" % q, tag="xh", align_bytes=64)
+            xhw = xh[:].rearrange("p h c e -> p (h c e)").bitcast(F32).rearrange("p (h c) -> p h c", h=2)
             for e in range(q * PAIR, (q + 1) * PAIR):
                 a = (e - q * PAIR) * C
                 for t in range(PACK):
                     nc.scalar.activation(
-                        xh[:, q, t // 2, a : a + C, t % 2], xbf[:, t, :].indirect(offs_t[:, e * cols : (e + 1) * cols]), COPY
+                        xh[:, t // 2, a : a + C, t % 2], xbf[:, t, :].indirect(offs_t[:, e * cols : (e + 1) * cols]), COPY
                     )
-            nc.scalar.copy(
-                xb[:, q, 1, :, :].rearrange("p c t -> p (c t)").bitcast(F32).rearrange("p (c h) -> p c h", h=2),
-                xh[:, q, :, :, :].rearrange("p h c e -> p (h c e)").bitcast(F32).rearrange("p (h c) -> p c h", h=2),
-            )
-        if TI_SPLIT:
-            for q in range(PAIRS):
-                nc.vector.tensor_copy(
-                    xb[:, q, 0, :, :].rearrange("p (c i) t -> p c t i", i=4),
-                    g4[:, :, q * PAIR * C : (q + 1) * PAIR * C].rearrange("p t (c i) -> p c t i", i=4),
+                if q == 1:
+                    nc.scalar.copy(
+                        xbe[:, BLOCK_OF[(e - q * PAIR, 1)], :, :].rearrange("p c t -> p (c t)").bitcast(F32).rearrange("p (c h) -> p c h", h=2),
+                        xhw[:, :, a : a + C].rearrange("p h c -> p c h"),
+                    )
+            if q == 0:
+                nc.scalar.copy(
+                    xb[:, q, 1, :, :].rearrange("p c t -> p (c t)").bitcast(F32).rearrange("p (c h) -> p c h", h=2),
+                    xhw.rearrange("p h c -> p c h"),
                 )
+        if TI_SPLIT:
+            nc.vector.tensor_copy(
+                xb[:, 0, 0, :, :].rearrange("p (c i) t -> p c t i", i=4),
+                g4[:, :, 0 : PAIR * C].rearrange("p t (c i) -> p c t i", i=4),
+            )
+            nc.vector.tensor_copy(
+                xbe[:, 1:3, :, :].rearrange("p b c t -> p (b c) t").rearrange("p (c i) t -> p c t i", i=4),
+                g4[:, :, PAIR * C : 2 * PAIR * C].rearrange("p t (c i) -> p c t i", i=4),
+            )
         else:
             nc.vector.tensor_copy(
                 xb[:, :, 0, :, :].rearrange("p q (c i) t -> p q c t i", i=4),
@@ -164,11 +176,13 @@ def tile_routed_moe_kernel(tc, xT, w, gate, offs, pos1, pos2, out):
 
         def quant_x(q):
             xc[q] = keep.tile([P, PASSES, PAIR * C], U32, name="xc%d" % q, tag=XC_TAGS[q], align_bytes=64)
-            nc.vector.quantize_mx(
-                out=xc[q][:].rearrange("p g c -> p (g c)").bitcast(FP8X4),
-                scales=xs[:, q, :, :].rearrange("p g c -> p (g c)"),
-                in_=xb[:, q, :, :, :].rearrange("p g c t -> p (g c t)"),
-            )
+            n = PASSES * PAIR * C // (2 if q == 1 else 1)
+            for k in range(2 if q == 1 else 1):
+                nc.vector.quantize_mx(
+                    out=xc[q][:].rearrange("p g c -> p (g c)")[:, k * n : (k + 1) * n].bitcast(FP8X4),
+                    scales=xs[:, q, :, :].rearrange("p g c -> p (g c)")[:, k * n : (k + 1) * n],
+                    in_=xb[:, q, :, :, :].rearrange("p g c t -> p (g c t)")[:, k * n * PACK : (k + 1) * n * PACK],
+                )
 
         for what, i in W_TEXT:
             if what == "lay":
@@ -188,8 +202,8 @@ def tile_routed_moe_kernel(tc, xT, w, gate, offs, pos1, pos2, out):
                         out=acc[:],
                         lhsT=wc[:, (e - e0) * PASSES + g, :].bitcast(FP8X4),
                         lhsT_scale=ws[:, (e - e0) * PASSES + g, :],
-                        rhs=xc[q][:, g, a : a + C].bitcast(FP8X4),
-                        rhs_scale=xs[:, q, g, a : a + C],
+                        rhs=(xc[q][:, g, a : a + C] if q == 0 else xc[q][:].rearrange("p g c -> p (g c)")[:, BLOCK_OF[(e % PAIR, g)] * C : (BLOCK_OF[(e % PAIR, g)] + 1) * C]).bitcast(FP8X4),
+                        rhs_scale=(xs[:, q, g, a : a + C] if q == 0 else xs[:, q, :, :].rearrange("p g c -> p (g c)")[:, BLOCK_OF[(e % PAIR, g)] * C : (BLOCK_OF[(e % PAIR, g)] + 1) * C]),
                         start=(g == 0),
                         stop=(g == PASSES - 1),
                     )

@@ -25,7 +25,7 @@ PAIR = 2
 PAIRS = E // PAIR
 WINDOW = 1024
 
-LOADS = [("p", 0), ("r", 0), ("p", 1), ("r", 1), ("r", 2), ("r", 3), ("p", 2), ("w", 0), ("p", 3), ("w", 1), ("w", 2), ("w", 3)]
+LOADS = [("p", 0), ("o", 0), ("r", 0), ("p", 1), ("r", 1), ("r", 2), ("r", 3), ("p", 2), ("w", 0), ("p", 3), ("w", 1), ("w", 2), ("w", 3)]
 CASTS = "SGGG"
 W_GROUPS = [(0, 0, 4, "wab", [("G", 0, 1), ("V", 1, 1), ("V", 2, 2)], "wc0"), (1, 0, 1, "wg2", [("G", 0, 1)], "xbf"), (1, 1, 2, "xbf", [("S", 0, 2)], "stage"), (1, 3, 1, "wv3", [("V", 0, 1)], "wc3")]
 XC_TAGS = ["xc0", "wab"]
@@ -54,7 +54,6 @@ def tile_routed_moe_kernel(tc, xT, w, gate, offs, pos1, pos2, out):
         psum = ctx.enter_context(tc.psum_pool(name="psum", bufs=1))
 
         offs_t = lists.tile([P, E * C // 16], U16, name="offs_t")
-        nc.sync.dma_start(offs_t[:], offs)
 
         ident = keep.tile([P, P], F32, name="ident")
         if PE_ADD:
@@ -65,7 +64,9 @@ def tile_routed_moe_kernel(tc, xT, w, gate, offs, pos1, pos2, out):
         raw1 = keep.tile([P, PACK, T], F32, name="raw1")
         w_raw = keep.tile([P, E * PASSES, PACK, N], F32, name="w_raw")
         for item in LOADS:
-            if item[0] == "p":
+            if item[0] == "o":
+                nc.sync.dma_start(offs_t[:], offs)
+            elif item[0] == "p":
                 nc.sync.dma_start(planes[item[1]][:, 0:T], x_view[0, :, item[1], :])
             elif item[0] == "r":
                 nc.sync.dma_start(raw1[:, item[1], :], x_view[1, :, item[1], :])

@@ -27,9 +27,10 @@ WINDOW = 1024
 
 LOADS = [("p", 0), ("o", 0), ("r", 0), ("p", 1), ("r", 1), ("r", 2), ("r", 3), ("p", 2), ("w", 0), ("p", 3), ("w", 1), ("w", 2), ("w", 3)]
 CASTS = "SGGG"
-W_GROUPS = [(0, 0, 4, "wab", [("G", 0, 1), ("V", 1, 1), ("V", 2, 2)], "wc0"), (1, 0, 1, "wg2", [("G", 0, 1)], "xbf"), (1, 1, 2, "xbf", [("S", 0, 2)], "stage"), (1, 3, 1, "wv3", [("V", 0, 1)], "wc3")]
+W_GROUPS = [(0, 0, 2, "wa", [("G", 0, 1), ("V", 1, 1)], "wc0"), (1, 0, 1, "wg2", [("G", 0, 1)], "xbf"), (1, 1, 2, "xbf", [("S", 0, 2)], "stage"), (1, 3, 1, "wv3", [("V", 0, 1)], "wc3"), (0, 2, 2, "wab", [("V", 0, 2)], "wc4")]
+MM_ORDER = [0, 4, 1, 2, 3]
 XC_TAGS = ["xc0", "wab"]
-W_TEXT = [("lay", 0), ("lay", 1), ("tq", 0), ("lay", 3), ("quant", 0), ("tq", 1), ("lay", 2), ("quant", 3), ("quant", 2), ("quant", 1)]
+W_TEXT = [("lay", 0), ("lay", 1), ("tq", 0), ("quant", 0), ("lay", 4), ("lay", 3), ("quant", 4), ("tq", 1), ("lay", 2), ("quant", 3), ("quant", 2), ("quant", 1)]
 PE_ADD = False
 RES_TAGS = ["gate0_1", "res1"]
 TI_SPLIT = True
@@ -193,7 +194,8 @@ def tile_routed_moe_kernel(tc, xT, w, gate, offs, pos1, pos2, out):
             else:
                 quant_x(i)
 
-        for i, (m, e0, ne, tag, cuts, ctag) in enumerate(W_GROUPS):
+        for i in MM_ORDER:
+            m, e0, ne, tag, cuts, ctag = W_GROUPS[i]
             wc, ws = wcs[i], wss[i]
             for e in range(e0, e0 + ne):
                 q, a = e // PAIR, (e % PAIR) * C

@@ -25,7 +25,7 @@ PAIR = 2
 PAIRS = E // PAIR
 WINDOW = 1024
 
-LOADS = [("p", 0), ("o", 0), ("r", 0), ("p", 1), ("r", 1), ("r", 2), ("r", 3), ("p", 2), ("w", 0), ("p", 3), ("w", 1), ("w", 2), ("w", 3)]
+LOADS = [("p", 0), ("o", 0), ("r", 0), ("p", 1), ("r", 1), ("r", 2), ("w", 0, 0), ("r", 3), ("p", 2), ("w", 0, 1), ("p", 3), ("w", 1), ("w", 2), ("w", 3)]
 CASTS = "SGGG"
 W_GROUPS = [(0, 0, 2, "wa", [("G", 0, 1), ("V", 1, 1)], "wc0"), (1, 0, 1, "wg2", [("G", 0, 1)], "xbf"), (1, 1, 2, "xbf", [("S", 0, 2)], "stage"), (1, 3, 1, "wv3", [("V", 0, 1)], "wc3"), (0, 2, 2, "wab", [("V", 0, 2)], "wc4")]
 MM_ORDER = [0, 4, 1, 2, 3]
@@ -156,7 +156,8 @@ def tile_routed_moe_kernel(tc, xT, w, gate, offs, pos1, pos2, out):
                 src = w_raw[:, (e0 + k0) * PASSES : (e0 + k0 + kn) * PASSES, :, m * P : (m + 1) * P]
                 dst = wbs[i][:, k0 * PASSES : (k0 + kn) * PASSES, :, :]
                 if eng == "G":
-                    move(eng, dst, src.rearrange("p u j n -> p u n j"))
+                    for u in range(kn * PASSES):
+                        move(eng, dst[:, u : u + 1, :, :], src[:, u : u + 1, :, :].rearrange("p u j n -> p u n j"))
                 else:
                     move(
                         eng,

@@ -25,9 +25,9 @@ PAIR = 2
 PAIRS = E // PAIR
 WINDOW = 1024
 
-LOADS = [("p", 0), ("o", 0), ("r", 0), ("p", 1), ("r", 1), ("r", 2), ("w", 0, 0), ("r", 3), ("p", 2), ("w", 0, 1), ("p", 3), ("w", 1), ("w", 2), ("w", 3)]
+LOADS = [("p", 0), ("o", 0), ("r", 0), ("p", 1), ("r", 1), ("r", 2), ("w", 0, 0), ("r", 3), ("p", 2), ("w", 0, 1), ("w", 1, 0), ("p", 3), ("w", 1, 1), ("w", 2), ("w", 3)]
 CASTS = "SGGG"
-W_GROUPS = [(0, 0, 2, "wa", [("G", 0, 1), ("V", 1, 1)], "wc0"), (1, 0, 1, "wg2", [("G", 0, 1)], "xbf"), (1, 1, 2, "xbf", [("S", 0, 2)], "stage"), (1, 3, 1, "wv3", [("V", 0, 1)], "wc3"), (0, 2, 2, "wab", [("V", 0, 2)], "wc4")]
+W_GROUPS = [(0, 0, 2, "wa", [("G", 0, 1), ("G", 1, 1)], "wc0"), (1, 0, 1, "wg2", [("G", 0, 1)], "xbf"), (1, 1, 2, "xbf", [("S", 0, 2)], "stage"), (1, 3, 1, "wv3", [("V", 0, 1)], "wc3"), (0, 2, 2, "wab", [("V", 0, 2)], "wc4")]
 MM_ORDER = [0, 4, 1, 2, 3]
 XC_TAGS = ["xc0", "wab"]
 W_TEXT = [("lay", 0), ("lay", 1), ("tq", 0), ("quant", 0), ("lay", 4), ("lay", 3), ("quant", 4), ("tq", 1), ("lay", 2), ("quant", 3), ("quant", 2), ("quant", 1)]

@@ -1,7 +1,6 @@
 from contextlib import ExitStack
 
 import concourse.mybir as mybir
-from concourse.masks import make_identity
 
 K, T, E, C, N = 1024, 512, 4, 256, 256
 FLOPS = 2 * K * N * E * C
@@ -23,224 +22,239 @@ PASSES = K // K_PASS
 BLOCKS = N // P
 PAIR = 2
 PAIRS = E // PAIR
-WINDOW = 1024
-
-LOADS = [("p", 0), ("o", 0), ("r", 0), ("p", 1), ("r", 1), ("r", 2), ("w", 0, 0), ("r", 3), ("p", 2), ("w", 0, 1), ("w", 1, 0), ("p", 3), ("w", 1, 1), ("w", 2), ("w", 3)]
-CASTS = "SGGG"
-W_GROUPS = [(0, 0, 2, "wa", [("G", 0, 1), ("G", 1, 1)], "wc0"), (1, 0, 1, "wg2", [("G", 0, 1)], "xbf"), (1, 1, 2, "xbf", [("S", 0, 2)], "stage"), (1, 3, 1, "wv3", [("V", 0, 1)], "wc3"), (0, 2, 2, "wab", [("V", 0, 2)], "wc4")]
-MM_ORDER = [0, 4, 1, 2, 3]
-XC_TAGS = ["xc0", "wab"]
-W_TEXT = [("lay", 0), ("lay", 1), ("tq", 0), ("quant", 0), ("lay", 4), ("lay", 3), ("quant", 4), ("tq", 1), ("lay", 2), ("quant", 3), ("quant", 2), ("quant", 1)]
-PE_ADD = False
-RES_TAGS = ["gate0_1", "res1"]
-TI_SPLIT = True
-TAIL_CUT = True
-BLOCK_OF = {(0, 1): 0, (0, 0): 1, (1, 0): 2, (1, 1): 3}
+WORD = 2
+WINDOW = 2 * T
+LIST_UNIT = 16
+LIST_COLS = C // LIST_UNIT
+RUN = 4
+HALF = T // 2
+ROUTES = 2
 
 
 def tile_routed_moe_kernel(tc, xT, w, gate, offs, pos1, pos2, out):
     nc = tc.nc
-
-    def move(eng, dst, src):
-        if eng == "S":
-            nc.scalar.copy(dst, src)
-        elif eng == "G":
-            nc.gpsimd.tensor_copy(dst, src)
-        else:
-            nc.vector.tensor_copy(dst, src)
 
     with ExitStack() as ctx:
         lists = ctx.enter_context(tc.tile_pool(name="lists", bufs=1))
         keep = ctx.enter_context(tc.tile_pool(name="keep", bufs=1))
         psum = ctx.enter_context(tc.psum_pool(name="psum", bufs=1))
 
-        offs_t = lists.tile([P, E * C // 16], U16, name="offs_t")
-
-        ident = keep.tile([P, P], F32, name="ident")
-        if PE_ADD:
-            make_identity(nc, ident[:])
-
-        x_view = xT.rearrange("(g p t) n -> g p t n", p=P, t=PACK)
-        planes = [keep.tile([P, WINDOW], F32, name="plane%d" % t) for t in range(PACK)]
-        raw1 = keep.tile([P, PACK, T], F32, name="raw1")
+        offs_t = lists.tile([P, E * LIST_COLS], U16, name="offs_t")
+        planes0 = [keep.tile([P, WINDOW], F32, name="plane0_%d" % t) for t in range(PACK)]
+        planes1 = keep.tile([P, PACK, T], F32, name="planes1")
         w_raw = keep.tile([P, E * PASSES, PACK, N], F32, name="w_raw")
-        for item in LOADS:
-            if item[0] == "o":
-                nc.sync.dma_start(offs_t[:], offs)
-            elif item[0] == "p":
-                nc.sync.dma_start(planes[item[1]][:, 0:T], x_view[0, :, item[1], :])
-            elif item[0] == "r":
-                nc.sync.dma_start(raw1[:, item[1], :], x_view[1, :, item[1], :])
-            elif len(item) == 2:
-                e = item[1]
-                nc.sync.dma_start(
-                    w_raw[:, e * PASSES : (e + 1) * PASSES, :, :].rearrange("p g j n -> p g (j n)"),
-                    w[e].rearrange("(g p j) n -> p g (j n)", p=P, j=PACK),
-                )
-            else:
-                e, g = item[1], item[2]
-                nc.sync.dma_start(
-                    w_raw[:, e * PASSES + g, :, :],
-                    w[e, g * K_PASS : (g + 1) * K_PASS, :].rearrange("(p j) n -> p j n", j=PACK),
-                )
+        x_view = xT.rearrange("(g p t) n -> g p t n", p=P, t=PACK)
 
-        pos1_t = lists.tile([P, T // 16], U16, name="pos1_t")
+        def load_plane0(t):
+            nc.sync.dma_start(planes0[t][:, 0:T], x_view[0, :, t, :])
+
+        def load_plane1(t):
+            nc.sync.dma_start(planes1[:, t, :], x_view[1, :, t, :])
+
+        def load_weights(e):
+            nc.sync.dma_start(
+                w_raw[:, e * PASSES : (e + 1) * PASSES, :, :].rearrange("p g j n -> p g (j n)"),
+                w[e].rearrange("(g p j) n -> p g (j n)", p=P, j=PACK),
+            )
+
+        def load_weights_of_pass(e, g):
+            nc.sync.dma_start(
+                w_raw[:, e * PASSES + g, :, :], w[e, g * K_PASS : (g + 1) * K_PASS, :].rearrange("(p j) n -> p j n", j=PACK)
+            )
+
+        load_plane0(0)
+        nc.sync.dma_start(offs_t[:], offs)
+        load_plane1(0)
+        load_plane0(1)
+        load_plane1(1)
+        load_plane1(2)
+        load_weights_of_pass(0, 0)
+        load_plane1(3)
+        load_plane0(2)
+        load_weights_of_pass(0, 1)
+        load_weights_of_pass(1, 0)
+        load_plane0(3)
+        load_weights_of_pass(1, 1)
+        load_weights(2)
+        load_weights(3)
+
+        pos1_t = lists.tile([P, T // LIST_UNIT], U16, name="pos1_t")
         nc.sync.dma_start(pos1_t[:], pos1)
-        pos2_t = lists.tile([P, T // 16], U16, name="pos2_t")
+        pos2_t = lists.tile([P, T // LIST_UNIT], U16, name="pos2_t")
         nc.sync.dma_start(pos2_t[:], pos2)
         pos_t = (pos1_t, pos2_t)
 
         gate_t = {}
         for m in range(BLOCKS):
-            for r in range(2):
-                gt = keep.tile([P, T], F32, name="gate%d_%d" % (r, m))
-                nc.sync.dma_start(gt[:], gate[r, m * P : (m + 1) * P, :])
-                gate_t[(r, m)] = gt
+            for r in range(ROUTES):
+                gate_t[(r, m)] = keep.tile([P, T], F32, name="gate%d_%d" % (r, m))
+                nc.sync.dma_start(gate_t[(r, m)][:], gate[r, m * P : (m + 1) * P, :])
 
-        xbf = keep.tile([P, PACK, T], BF16, name="xbf", tag="xbf", align_bytes=64)
-        for t in range(PACK):
-            move(CASTS[t], xbf[:, t, :], raw1[:, t, :])
+        cast1 = keep.tile([P, PACK, T], BF16, name="cast1", tag="cast1", align_bytes=64)
+        nc.scalar.copy(cast1[:, 0, :], planes1[:, 0, :])
+        for t in range(1, PACK):
+            nc.gpsimd.tensor_copy(cast1[:, t, :], planes1[:, t, :])
 
-        y_sb = [keep.tile([P, E * C], F32, name="y_sb%d" % m) for m in range(BLOCKS)]
+        sums = [keep.tile([P, E * C], F32, name="sums%d" % m) for m in range(BLOCKS)]
 
-        cols = C // 16
-        xb = keep.tile([P, PAIRS, PASSES, PAIR * C, PACK], BF16, name="xb", tag="stage", align_bytes=64)
-        xs = keep.tile([P, PAIRS, PASSES, PAIR * C], U8, name="xs", align_bytes=64)
-        g4 = keep.tile([P, PACK, E * C], F32, name="g4")
-        xbe = xb[:, 1, :, :, :].rearrange("p g c t -> p (g c t)").rearrange("p (b c t) -> p b c t", b=PAIR * PASSES, t=PACK)
+        tokens = keep.tile([P, PAIRS, PASSES, PAIR * C, PACK], BF16, name="tokens", tag="tokens", align_bytes=64)
+        token_scales = keep.tile([P, PAIRS, PASSES, PAIR * C], U8, name="token_scales", align_bytes=64)
+        runs23 = tokens[:, 1, :, :, :].rearrange("p g c t -> p (g c t)").rearrange("p (b c t) -> p b c t", b=PAIR * PASSES, t=PACK)
+        run_of = {(2, 1): 0, (2, 0): 1, (3, 0): 2, (3, 1): 3}
+
+        gathered0 = keep.tile([P, PACK, E * C], F32, name="gathered0")
         for q in range(PAIRS):
             for t in range(PACK):
                 nc.vector.tensor_copy(
-                    g4[:, t, q * PAIR * C : (q + 1) * PAIR * C],
-                    planes[t][:].indirect(offs_t[:, q * PAIR * cols : (q + 1) * PAIR * cols]),
+                    gathered0[:, t, q * PAIR * C : (q + 1) * PAIR * C],
+                    planes0[t][:].indirect(offs_t[:, q * PAIR * LIST_COLS : (q + 1) * PAIR * LIST_COLS]),
                 )
-            xh = keep.tile([P, 2, PAIR * C, 2], BF16, name="xh%d" % q, tag="xh", align_bytes=64)
-            xhw = xh[:].rearrange("p h c e -> p (h c e)").bitcast(F32).rearrange("p (h c) -> p h c", h=2)
+            pairs1 = keep.tile([P, PACK // WORD, PAIR * C, WORD], BF16, name="pairs1_%d" % q, tag="pairs1", align_bytes=64)
+            words1 = pairs1[:].rearrange("p h c e -> p (h c e)").bitcast(F32).rearrange("p (h c) -> p h c", h=PACK // WORD)
             for e in range(q * PAIR, (q + 1) * PAIR):
                 a = (e - q * PAIR) * C
                 for t in range(PACK):
                     nc.scalar.activation(
-                        xh[:, t // 2, a : a + C, t % 2], xbf[:, t, :].indirect(offs_t[:, e * cols : (e + 1) * cols]), COPY
+                        pairs1[:, t // WORD, a : a + C, t % WORD],
+                        cast1[:, t, :].indirect(offs_t[:, e * LIST_COLS : (e + 1) * LIST_COLS]),
+                        COPY,
                     )
                 if q == 1:
                     nc.scalar.copy(
-                        xbe[:, BLOCK_OF[(e - q * PAIR, 1)], :, :].rearrange("p c t -> p (c t)").bitcast(F32).rearrange("p (c h) -> p c h", h=2),
-                        xhw[:, :, a : a + C].rearrange("p h c -> p c h"),
+                        runs23[:, run_of[(e, 1)], :, :].rearrange("p c t -> p (c t)").bitcast(F32).rearrange("p (c h) -> p c h", h=PACK // WORD),
+                        words1[:, :, a : a + C].rearrange("p h c -> p c h"),
                     )
             if q == 0:
                 nc.scalar.copy(
-                    xb[:, q, 1, :, :].rearrange("p c t -> p (c t)").bitcast(F32).rearrange("p (c h) -> p c h", h=2),
-                    xhw.rearrange("p h c -> p c h"),
-                )
-        if TI_SPLIT:
-            nc.vector.tensor_copy(
-                xb[:, 0, 0, :, :].rearrange("p (c i) t -> p c t i", i=4),
-                g4[:, :, 0 : PAIR * C].rearrange("p t (c i) -> p c t i", i=4),
-            )
-            nc.vector.tensor_copy(
-                xbe[:, 1:3, :, :].rearrange("p b c t -> p (b c) t").rearrange("p (c i) t -> p c t i", i=4),
-                g4[:, :, PAIR * C : 2 * PAIR * C].rearrange("p t (c i) -> p c t i", i=4),
-            )
-        else:
-            nc.vector.tensor_copy(
-                xb[:, :, 0, :, :].rearrange("p q (c i) t -> p q c t i", i=4),
-                g4[:].rearrange("p t (q c i) -> p q c t i", q=PAIRS, i=4),
-            )
-
-        wbs, wcs, wss = {}, {}, {}
-
-        def lay(i):
-            m, e0, ne, tag, cuts, ctag = W_GROUPS[i]
-            wbs[i] = keep.tile([P, ne * PASSES, P, PACK], BF16, name="wb%d" % i, tag=tag, align_bytes=64)
-            for eng, k0, kn in cuts:
-                src = w_raw[:, (e0 + k0) * PASSES : (e0 + k0 + kn) * PASSES, :, m * P : (m + 1) * P]
-                dst = wbs[i][:, k0 * PASSES : (k0 + kn) * PASSES, :, :]
-                if eng == "G":
-                    for u in range(kn * PASSES):
-                        move(eng, dst[:, u : u + 1, :, :], src[:, u : u + 1, :, :].rearrange("p u j n -> p u n j"))
-                else:
-                    move(
-                        eng,
-                        dst.rearrange("p u (c i) j -> p u c j i", i=4),
-                        src.rearrange("p u j (c i) -> p u c j i", i=4),
-                    )
-
-        def quant_w(i):
-            m, e0, ne, tag, cuts, ctag = W_GROUPS[i]
-            wcs[i] = keep.tile([P, ne * PASSES, P], U32, name="wc%d" % i, tag=ctag, align_bytes=64)
-            wss[i] = keep.tile([P, ne * PASSES, P], U8, name="ws%d" % i, align_bytes=64)
-            nc.vector.quantize_mx(
-                out=wcs[i][:].rearrange("p u n -> p (u n)").bitcast(FP8X4),
-                scales=wss[i][:].rearrange("p u n -> p (u n)"),
-                in_=wbs[i][:].rearrange("p u n j -> p (u n j)"),
-            )
-
-        xc = {}
-
-        def quant_x(q):
-            xc[q] = keep.tile([P, PASSES, PAIR * C], U32, name="xc%d" % q, tag=XC_TAGS[q], align_bytes=64)
-            n = PASSES * PAIR * C // (2 if q == 1 else 1)
-            for k in range(2 if q == 1 else 1):
-                nc.vector.quantize_mx(
-                    out=xc[q][:].rearrange("p g c -> p (g c)")[:, k * n : (k + 1) * n].bitcast(FP8X4),
-                    scales=xs[:, q, :, :].rearrange("p g c -> p (g c)")[:, k * n : (k + 1) * n],
-                    in_=xb[:, q, :, :, :].rearrange("p g c t -> p (g c t)")[:, k * n * PACK : (k + 1) * n * PACK],
+                    tokens[:, 0, 1, :, :].rearrange("p c t -> p (c t)").bitcast(F32).rearrange("p (c h) -> p c h", h=PACK // WORD),
+                    words1.rearrange("p h c -> p c h"),
                 )
 
-        for what, i in W_TEXT:
-            if what == "lay":
-                lay(i)
-            elif what == "quant":
-                quant_w(i)
+        nc.vector.tensor_copy(
+            tokens[:, 0, 0, :, :].rearrange("p (c i) t -> p c t i", i=RUN),
+            gathered0[:, :, 0 : PAIR * C].rearrange("p t (c i) -> p c t i", i=RUN),
+        )
+        nc.vector.tensor_copy(
+            runs23[:, run_of[(2, 0)] : run_of[(3, 0)] + 1, :, :].rearrange("p b c t -> p (b c) t").rearrange("p (c i) t -> p c t i", i=RUN),
+            gathered0[:, :, PAIR * C : 2 * PAIR * C].rearrange("p t (c i) -> p c t i", i=RUN),
+        )
+
+        def stage_weights(name, tag, experts):
+            return keep.tile([P, experts * PASSES, P, PACK], BF16, name=name, tag=tag, align_bytes=64)
+
+        def interleave_weights(engine, staged, at, m, e, experts):
+            src = w_raw[:, e * PASSES : (e + experts) * PASSES, :, m * P : (m + 1) * P]
+            dst = staged[:, at * PASSES : (at + experts) * PASSES, :, :]
+            if engine == "gpsimd":
+                for u in range(experts * PASSES):
+                    nc.gpsimd.tensor_copy(dst[:, u : u + 1, :, :], src[:, u : u + 1, :, :].rearrange("p u j n -> p u n j"))
+                return
+            dst = dst.rearrange("p u (c i) j -> p u c j i", i=RUN)
+            src = src.rearrange("p u j (c i) -> p u c j i", i=RUN)
+            if engine == "scalar":
+                nc.scalar.copy(dst, src)
             else:
-                quant_x(i)
+                nc.vector.tensor_copy(dst, src)
 
-        for i in MM_ORDER:
-            m, e0, ne, tag, cuts, ctag = W_GROUPS[i]
-            wc, ws = wcs[i], wss[i]
-            for e in range(e0, e0 + ne):
-                q, a = e // PAIR, (e % PAIR) * C
+        def quantize_weights(name, tag, staged, experts):
+            codes = keep.tile([P, experts * PASSES, P], U32, name=name + "_codes", tag=tag, align_bytes=64)
+            scales = keep.tile([P, experts * PASSES, P], U8, name=name + "_scales", align_bytes=64)
+            nc.vector.quantize_mx(
+                out=codes[:].rearrange("p u n -> p (u n)").bitcast(FP8X4),
+                scales=scales[:].rearrange("p u n -> p (u n)"),
+                in_=staged[:].rearrange("p u n j -> p (u n j)"),
+            )
+            return codes, scales
+
+        def quantize_tokens(codes, first, runs):
+            nc.vector.quantize_mx(
+                out=codes.bitcast(FP8X4),
+                scales=token_scales[:].rearrange("p q g c -> p (q g c)")[:, first * C : (first + runs) * C],
+                in_=tokens[:].rearrange("p q g c t -> p (q g c t)")[:, first * C * PACK : (first + runs) * C * PACK],
+            )
+
+        staged_b0_e01 = stage_weights("staged_b0_e01", "staged_b0_e01", 2)
+        interleave_weights("gpsimd", staged_b0_e01, 0, 0, 0, 1)
+        interleave_weights("gpsimd", staged_b0_e01, 1, 0, 1, 1)
+        staged_b1_e0 = stage_weights("staged_b1_e0", "staged_b1_e0", 1)
+        interleave_weights("gpsimd", staged_b1_e0, 0, 1, 0, 1)
+
+        codes01 = keep.tile([P, PASSES, PAIR * C], U32, name="codes01", align_bytes=64)
+        quantize_tokens(codes01[:].rearrange("p g c -> p (g c)"), 0, PAIR * PASSES)
+        w_b0_e01 = quantize_weights("w_b0_e01", "w_b0_e01", staged_b0_e01, 2)
+
+        staged_b0_e23 = stage_weights("staged_b0_e23", "staged_b0_e23", 2)
+        interleave_weights("vector", staged_b0_e23, 0, 0, 2, 2)
+        staged_b1_e3 = stage_weights("staged_b1_e3", "staged_b1_e3", 1)
+        interleave_weights("vector", staged_b1_e3, 0, 1, 3, 1)
+        w_b0_e23 = quantize_weights("w_b0_e23", "w_b0_e23", staged_b0_e23, 2)
+
+        codes23 = keep.tile([P, PASSES, PAIR * C], U32, name="codes23", tag="staged_b0_e23", align_bytes=64)
+        codes23_runs = codes23[:].rearrange("p g c -> p (g c)")
+        for e in range(PAIR, E):
+            at = (e - PAIR) * PASSES
+            quantize_tokens(codes23_runs[:, at * C : (at + PASSES) * C], PAIR * PASSES + at, PASSES)
+
+        staged_b1_e12 = stage_weights("staged_b1_e12", "cast1", 2)
+        interleave_weights("scalar", staged_b1_e12, 0, 1, 1, 2)
+
+        w_b1_e3 = quantize_weights("w_b1_e3", "w_b1_e3", staged_b1_e3, 1)
+        w_b1_e12 = quantize_weights("w_b1_e12", "tokens", staged_b1_e12, 2)
+        w_b1_e0 = quantize_weights("w_b1_e0", "cast1", staged_b1_e0, 1)
+
+        def token_operand(e, g):
+            if e < PAIR:
+                return codes01[:, g, e * C : (e + 1) * C], token_scales[:, 0, g, e * C : (e + 1) * C]
+            b = run_of[(e, g)]
+            return (
+                codes23_runs[:, b * C : (b + 1) * C],
+                token_scales[:, 1, :, :].rearrange("p g c -> p (g c)")[:, b * C : (b + 1) * C],
+            )
+
+        def multiply(m, experts, piece):
+            codes, scales = piece
+            for i, e in enumerate(experts):
                 acc = psum.tile([P, C], F32, name="acc%d_%d" % (e, m))
                 for g in range(PASSES):
+                    rhs, rhs_scale = token_operand(e, g)
                     nc.tensor.matmul_mx(
                         out=acc[:],
-                        lhsT=wc[:, (e - e0) * PASSES + g, :].bitcast(FP8X4),
-                        lhsT_scale=ws[:, (e - e0) * PASSES + g, :],
-                        rhs=(xc[q][:, g, a : a + C] if q == 0 else xc[q][:].rearrange("p g c -> p (g c)")[:, BLOCK_OF[(e % PAIR, g)] * C : (BLOCK_OF[(e % PAIR, g)] + 1) * C]).bitcast(FP8X4),
-                        rhs_scale=(xs[:, q, g, a : a + C] if q == 0 else xs[:, q, :, :].rearrange("p g c -> p (g c)")[:, BLOCK_OF[(e % PAIR, g)] * C : (BLOCK_OF[(e % PAIR, g)] + 1) * C]),
+                        lhsT=codes[:, i * PASSES + g, :].bitcast(FP8X4),
+                        lhsT_scale=scales[:, i * PASSES + g, :],
+                        rhs=rhs.bitcast(FP8X4),
+                        rhs_scale=rhs_scale,
                         start=(g == 0),
                         stop=(g == PASSES - 1),
                     )
-                nc.scalar.copy(y_sb[m][:, e * C : (e + 1) * C], acc[:])
+                nc.scalar.copy(sums[m][:, e * C : (e + 1) * C], acc[:])
 
-        for m in range(BLOCKS):
-            parts = []
-            cut = TAIL_CUT and m == BLOCKS - 1
-            for r in range(2):
-                part = keep.tile([P, T], F32, name="part%d_%d" % (r, m))
-                if cut and r == 1:
-                    for h in range(2):
-                        nc.vector.tensor_tensor(
-                            part[:, h * (T // 2) : (h + 1) * (T // 2)],
-                            y_sb[m][:].indirect(pos_t[r][:, h * (T // 32) : (h + 1) * (T // 32)]),
-                            gate_t[(r, m)][:, h * (T // 2) : (h + 1) * (T // 2)],
-                            MULT,
-                        )
-                else:
-                    nc.vector.tensor_tensor(part[:], y_sb[m][:].indirect(pos_t[r][:]), gate_t[(r, m)][:], MULT)
-                parts.append(part)
-            res = keep.tile([P, T], F32, name="res%d" % m, tag=RES_TAGS[m])
-            if cut:
-                for h in range(2):
-                    hs = slice(h * (T // 2), (h + 1) * (T // 2))
-                    nc.vector.tensor_tensor(res[:, hs], parts[0][:, hs], parts[1][:, hs], ADD)
-                    nc.sync.dma_start(out[m * P : (m + 1) * P, hs], res[:, hs])
-                continue
-            if PE_ADD and m == 0:
-                total = psum.tile([P, T], F32, name="total", tag="acc%d_%d" % (E - 1, BLOCKS - 1))
-                nc.tensor.matmul(total[:], lhsT=ident[:], rhs=parts[0][:], start=True, stop=False)
-                nc.tensor.matmul(total[:], lhsT=ident[:], rhs=parts[1][:], start=False, stop=True)
-                nc.scalar.copy(res[:], total[:])
-            else:
-                nc.vector.tensor_tensor(res[:], parts[0][:], parts[1][:], ADD)
-            nc.sync.dma_start(out[m * P : (m + 1) * P, :], res[:])
+        multiply(0, (0, 1), w_b0_e01)
+        multiply(0, (2, 3), w_b0_e23)
+        multiply(1, (0,), w_b1_e0)
+        multiply(1, (1, 2), w_b1_e12)
+        multiply(1, (3,), w_b1_e3)
+
+        def fetch(part, m, r, t0, t1):
+            nc.vector.tensor_tensor(
+                part[:, t0:t1], sums[m][:].indirect(pos_t[r][:, t0 // LIST_UNIT : t1 // LIST_UNIT]), gate_t[(r, m)][:, t0:t1], MULT
+            )
+
+        def add_and_store(result, parts, m, t0, t1):
+            nc.vector.tensor_tensor(result[:, t0:t1], parts[0][:, t0:t1], parts[1][:, t0:t1], ADD)
+            nc.sync.dma_start(out[m * P : (m + 1) * P, t0:t1], result[:, t0:t1])
+
+        parts0 = []
+        for r in range(ROUTES):
+            parts0.append(keep.tile([P, T], F32, name="part%d_0" % r))
+            fetch(parts0[r], 0, r, 0, T)
+        result0 = keep.tile([P, T], F32, name="result0", tag="gate0_1")
+        add_and_store(result0, parts0, 0, 0, T)
+
+        parts1 = [keep.tile([P, T], F32, name="part0_1")]
+        fetch(parts1[0], 1, 0, 0, T)
+        parts1.append(keep.tile([P, T], F32, name="part1_1"))
+        for t0 in (0, HALF):
+            fetch(parts1[1], 1, 1, t0, t0 + HALF)
+        result1 = keep.tile([P, T], F32, name="result1")
+        for t0 in (0, HALF):
+            add_and_store(result1, parts1, 1, t0, t0 + HALF)

@@ -109,26 +109,40 @@ def tile_routed_moe_kernel(tc, xT, w, gate, offs, pos1, pos2, out):
                     gathered0[:, t, q * PAIR * C : (q + 1) * PAIR * C],
                     planes0[t][:].indirect(offs_t[:, q * PAIR * LIST_COLS : (q + 1) * PAIR * LIST_COLS]),
                 )
-            pairs1 = keep.tile([P, PACK // WORD, PAIR * C, WORD], BF16, name="pairs1_%d" % q, tag="pairs1", align_bytes=64)
-            words1 = pairs1[:].rearrange("p h c e -> p (h c e)").bitcast(F32).rearrange("p (h c) -> p h c", h=PACK // WORD)
-            for e in range(q * PAIR, (q + 1) * PAIR):
-                a = (e - q * PAIR) * C
-                for t in range(PACK):
-                    nc.scalar.activation(
-                        pairs1[:, t // WORD, a : a + C, t % WORD],
-                        cast1[:, t, :].indirect(offs_t[:, e * LIST_COLS : (e + 1) * LIST_COLS]),
-                        COPY,
-                    )
-                if q == 1:
-                    nc.scalar.copy(
-                        runs23[:, run_of[(e, 1)], :, :].rearrange("p c t -> p (c t)").bitcast(F32).rearrange("p (c h) -> p c h", h=PACK // WORD),
-                        words1[:, :, a : a + C].rearrange("p h c -> p c h"),
-                    )
-            if q == 0:
-                nc.scalar.copy(
-                    tokens[:, 0, 1, :, :].rearrange("p c t -> p (c t)").bitcast(F32).rearrange("p (c h) -> p c h", h=PACK // WORD),
-                    words1.rearrange("p h c -> p c h"),
-                )
+
+        pairs1 = {}
+
+        def pairs_tile(e):
+            pairs1[e] = keep.tile([P, PACK // WORD, C, WORD], BF16, name="pairs1_%d" % e, tag="pairs1_%d" % (e % PAIR), align_bytes=64)
+
+        def gather1(e, t):
+            nc.scalar.activation(
+                pairs1[e][:, t // WORD, :, t % WORD], cast1[:, t, :].indirect(offs_t[:, e * LIST_COLS : (e + 1) * LIST_COLS]), COPY
+            )
+
+        def weave1(e):
+            run = tokens[:, 0, 1, e * C : (e + 1) * C, :] if e < PAIR else runs23[:, run_of[(e, 1)], :, :]
+            nc.scalar.copy(
+                run.rearrange("p c t -> p (c t)").bitcast(F32).rearrange("p (c h) -> p c h", h=PACK // WORD),
+                pairs1[e][:].rearrange("p h c e -> p (h c e)").bitcast(F32).rearrange("p (h c) -> p c h", h=PACK // WORD),
+            )
+
+        pairs_tile(0)
+        pairs_tile(1)
+        for t in range(PACK):
+            gather1(0, t)
+            gather1(1, t)
+        weave1(0)
+        weave1(1)
+        pairs_tile(2)
+        pairs_tile(3)
+        for t in (0, 2, 1, 3):
+            gather1(2, t)
+        gather1(3, 0)
+        weave1(2)
+        for t in (2, 1, 3):
+            gather1(3, t)
+        weave1(3)
 
         nc.vector.tensor_copy(
             tokens[:, 0, 0, :, :].rearrange("p (c i) t -> p c t i", i=RUN),

@@ -40,7 +40,7 @@ def tile_routed_moe_kernel(tc, xT, w, gate, offs, pos1, pos2, out):
         psum = ctx.enter_context(tc.psum_pool(name="psum", bufs=1))
 
         offs_t = lists.tile([P, E * LIST_COLS], U16, name="offs_t")
-        planes0 = [keep.tile([P, WINDOW], F32, name="plane0_%d" % t) for t in range(PACK)]
+        planes0 = [keep.tile([P, T], F32, name="plane0_%d" % t) for t in range(PACK)]
         planes1 = keep.tile([P, PACK, T], F32, name="planes1")
         w_raw = keep.tile([P, E * PASSES, PACK, N], F32, name="w_raw")
         x_view = xT.rearrange("(g p t) n -> g p t n", p=P, t=PACK)
@@ -102,12 +102,13 @@ def tile_routed_moe_kernel(tc, xT, w, gate, offs, pos1, pos2, out):
         runs23 = tokens[:, 1, :, :, :].rearrange("p g c t -> p (g c t)").rearrange("p (b c t) -> p b c t", b=PAIR * PASSES, t=PACK)
         run_of = {(2, 1): 0, (2, 0): 1, (3, 0): 2, (3, 1): 3}
 
-        gathered0 = keep.tile([P, PACK, E * C], F32, name="gathered0")
-        for q in range(PAIRS):
-            for t in range(PACK):
+        pairs0 = [keep.tile([P, PACK // WORD, PAIR * C, WORD], BF16, name="pairs0_%d" % q, align_bytes=64) for q in range(PAIRS)]
+        for t in range(PACK):
+            for e in range(E):
+                a = (e % PAIR) * C
                 nc.vector.tensor_copy(
-                    gathered0[:, t, q * PAIR * C : (q + 1) * PAIR * C],
-                    planes0[t][:].indirect(offs_t[:, q * PAIR * LIST_COLS : (q + 1) * PAIR * LIST_COLS]),
+                    pairs0[e // PAIR][:, t // WORD, a : a + C, t % WORD],
+                    planes0[t][:].indirect(offs_t[:, e * LIST_COLS : (e + 1) * LIST_COLS]),
                 )
 
         pairs1 = {}
@@ -144,14 +145,14 @@ def tile_routed_moe_kernel(tc, xT, w, gate, offs, pos1, pos2, out):
             gather1(3, t)
         weave1(3)
 
-        nc.vector.tensor_copy(
-            tokens[:, 0, 0, :, :].rearrange("p (c i) t -> p c t i", i=RUN),
-            gathered0[:, :, 0 : PAIR * C].rearrange("p t (c i) -> p c t i", i=RUN),
-        )
-        nc.vector.tensor_copy(
-            runs23[:, run_of[(2, 0)] : run_of[(3, 0)] + 1, :, :].rearrange("p b c t -> p (b c) t").rearrange("p (c i) t -> p c t i", i=RUN),
-            gathered0[:, :, PAIR * C : 2 * PAIR * C].rearrange("p t (c i) -> p c t i", i=RUN),
-        )
+        def weave0(q, run):
+            nc.vector.tensor_copy(
+                run.bitcast(F32).rearrange("p (c h) -> p c h", h=PACK // WORD),
+                pairs0[q][:].rearrange("p h c e -> p (h c e)").bitcast(F32).rearrange("p (h c) -> p c h", h=PACK // WORD),
+            )
+
+        weave0(0, tokens[:, 0, 0, :, :].rearrange("p c t -> p (c t)"))
+        weave0(1, runs23[:, run_of[(2, 0)] : run_of[(3, 0)] + 1, :, :].rearrange("p b c t -> p (b c t)"))
 
         def stage_weights(name, tag, experts):
             return keep.tile([P, experts * PASSES, P, PACK], BF16, name=name, tag=tag, align_bytes=64)

@@ -38,6 +38,7 @@ def tile_routed_moe_kernel(tc, xT, w, gate, offs, pos1, pos2, out):
         lists = ctx.enter_context(tc.tile_pool(name="lists", bufs=1))
         keep = ctx.enter_context(tc.tile_pool(name="keep", bufs=1))
         psum = ctx.enter_context(tc.psum_pool(name="psum", bufs=1))
+        placed = ctx.enter_context(tc.tile_pool(name="placed", bufs=1))
 
         offs_t = lists.tile([P, E * LIST_COLS], U16, name="offs_t")
         planes0 = [keep.tile([P, T], F32, name="plane0_%d" % t) for t in range(PACK)]
@@ -171,13 +172,16 @@ def tile_routed_moe_kernel(tc, xT, w, gate, offs, pos1, pos2, out):
             else:
                 nc.vector.tensor_copy(dst, src)
 
-        def quantize_weights(name, tag, staged, experts):
-            codes = keep.tile([P, experts * PASSES, P], U32, name=name + "_codes", tag=tag, align_bytes=64)
+        def quantize_weights(name, tag, staged, experts, at_byte=None):
+            if at_byte is None:
+                codes = keep.tile([P, experts * PASSES, P], U32, name=name + "_codes", tag=tag, align_bytes=64)
+            else:
+                codes = placed.tile([P, experts * PASSES, P], U32, name=name + "_codes", offset=at_byte, align_bytes=64)
             scales = keep.tile([P, experts * PASSES, P], U8, name=name + "_scales", align_bytes=64)
             nc.vector.quantize_mx(
                 out=codes[:].rearrange("p u n -> p (u n)").bitcast(FP8X4),
                 scales=scales[:].rearrange("p u n -> p (u n)"),
-                in_=staged[:].rearrange("p u n j -> p (u n j)"),
+                in_=staged[:, 0 : experts * PASSES, :, :].rearrange("p u n j -> p (u n j)"),
             )
             return codes, scales
 
@@ -198,13 +202,13 @@ def tile_routed_moe_kernel(tc, xT, w, gate, offs, pos1, pos2, out):
         quantize_tokens(codes01[:].rearrange("p g c -> p (g c)"), 0, PAIR * PASSES)
         w_b0_e01 = quantize_weights("w_b0_e01", "w_b0_e01", staged_b0_e01, 2)
 
-        staged_b0_e23 = stage_weights("staged_b0_e23", "staged_b0_e23", 2)
+        staged_b0_e23 = placed.tile([P, 7, P, PACK], BF16, name="staged_b0_e23", offset=0, align_bytes=64)
         interleave_weights("vector", staged_b0_e23, 0, 0, 2, 2)
         staged_b1_e3 = stage_weights("staged_b1_e3", "staged_b1_e3", 1)
         interleave_weights("vector", staged_b1_e3, 0, 1, 3, 1)
         w_b0_e23 = quantize_weights("w_b0_e23", "w_b0_e23", staged_b0_e23, 2)
 
-        codes23 = keep.tile([P, PASSES, PAIR * C], U32, name="codes23", tag="staged_b0_e23", align_bytes=64)
+        codes23 = placed.tile([P, PASSES, PAIR * C], U32, name="codes23", offset=0, align_bytes=64)
         codes23_runs = codes23[:].rearrange("p g c -> p (g c)")
         for e in range(PAIR, E):
             at = (e - PAIR) * PASSES
@@ -214,8 +218,8 @@ def tile_routed_moe_kernel(tc, xT, w, gate, offs, pos1, pos2, out):
         interleave_weights("scalar", staged_b1_e12, 0, 1, 1, 2)
 
         w_b1_e3 = quantize_weights("w_b1_e3", "w_b1_e3", staged_b1_e3, 1)
-        w_b1_e12 = quantize_weights("w_b1_e12", "tokens", staged_b1_e12, 2)
-        w_b1_e0 = quantize_weights("w_b1_e0", "cast1", staged_b1_e0, 1)
+        w_b1_e0 = quantize_weights("w_b1_e0", "", staged_b1_e0, 1, at_byte=4096)
+        w_b1_e12 = quantize_weights("w_b1_e12", "", staged_b1_e12, 2, at_byte=5120)
 
         def token_operand(e, g):
             if e < PAIR:

@@ -202,10 +202,17 @@ def tile_routed_moe_kernel(tc, xT, w, gate, offs, pos1, pos2, out):
         quantize_tokens(codes01[:].rearrange("p g c -> p (g c)"), 0, PAIR * PASSES)
         w_b0_e01 = quantize_weights("w_b0_e01", "w_b0_e01", staged_b0_e01, 2)
 
-        staged_b0_e23 = placed.tile([P, 7, P, PACK], BF16, name="staged_b0_e23", offset=0, align_bytes=64)
+        staged_b0_e23 = placed.tile([P, 8, P, PACK], BF16, name="staged_b0_e23", offset=0, align_bytes=64)
         interleave_weights("vector", staged_b0_e23, 0, 0, 2, 2)
-        staged_b1_e3 = stage_weights("staged_b1_e3", "staged_b1_e3", 1)
-        interleave_weights("vector", staged_b1_e3, 0, 1, 3, 1)
+        staged_b1_e123 = keep.tile([P, 3 * PASSES, P, PACK], BF16, name="staged_b1_e123", align_bytes=64)
+        nc.vector.tensor_copy(
+            staged_b1_e123[:, 4:6, :, :].rearrange("p u (c i) j -> p u c j i", i=RUN),
+            w_raw[:, 6:8, :, P : 2 * P].rearrange("p u j (c i) -> p u c j i", i=RUN),
+        )
+        nc.vector.tensor_copy(
+            staged_b1_e123[:, 3, :, :].rearrange("p (c i) j -> p c j i", i=RUN),
+            w_raw[:, 5, :, P : 2 * P].rearrange("p j (c i) -> p c j i", i=RUN),
+        )
         w_b0_e23 = quantize_weights("w_b0_e23", "w_b0_e23", staged_b0_e23, 2)
 
         codes23 = placed.tile([P, PASSES, PAIR * C], U32, name="codes23", offset=0, align_bytes=64)
@@ -214,12 +221,14 @@ def tile_routed_moe_kernel(tc, xT, w, gate, offs, pos1, pos2, out):
             at = (e - PAIR) * PASSES
             quantize_tokens(codes23_runs[:, at * C : (at + PASSES) * C], PAIR * PASSES + at, PASSES)
 
-        staged_b1_e12 = stage_weights("staged_b1_e12", "cast1", 2)
-        interleave_weights("scalar", staged_b1_e12, 0, 1, 1, 2)
+        nc.scalar.copy(
+            staged_b1_e123[:, 0:3, :, :].rearrange("p u (c i) j -> p u c j i", i=RUN),
+            w_raw[:, 2:5, :, P : 2 * P].rearrange("p u j (c i) -> p u c j i", i=RUN),
+        )
 
-        w_b1_e3 = quantize_weights("w_b1_e3", "w_b1_e3", staged_b1_e3, 1)
+        w_b1_e3 = quantize_weights("w_b1_e3", "", staged_b1_e123[:, 4:6, :, :], 1, at_byte=7168)
         w_b1_e0 = quantize_weights("w_b1_e0", "", staged_b1_e0, 1, at_byte=4096)
-        w_b1_e12 = quantize_weights("w_b1_e12", "", staged_b1_e12, 2, at_byte=5120)
+        w_b1_e12 = quantize_weights("w_b1_e12", "", staged_b1_e123, 2, at_byte=5120)
 
         def token_operand(e, g):
             if e < PAIR:
@@ -230,14 +239,15 @@ def tile_routed_moe_kernel(tc, xT, w, gate, offs, pos1, pos2, out):
                 token_scales[:, 1, :, :].rearrange("p g c -> p (g c)")[:, b * C : (b + 1) * C],
             )
 
-        def multiply(m, experts, piece):
+        def multiply(m, experts, piece, together=False):
             codes, scales = piece
+            bank = psum.tile([P, len(experts) * C], F32, name="bank%d_%d" % (experts[0], m)) if together else None
             for i, e in enumerate(experts):
-                acc = psum.tile([P, C], F32, name="acc%d_%d" % (e, m))
+                acc = bank[:, i * C : (i + 1) * C] if together else psum.tile([P, C], F32, name="acc%d_%d" % (e, m))[:]
                 for g in range(PASSES):
                     rhs, rhs_scale = token_operand(e, g)
                     nc.tensor.matmul_mx(
-                        out=acc[:],
+                        out=acc,
                         lhsT=codes[:, i * PASSES + g, :].bitcast(FP8X4),
                         lhsT_scale=scales[:, i * PASSES + g, :],
                         rhs=rhs.bitcast(FP8X4),
@@ -245,9 +255,12 @@ def tile_routed_moe_kernel(tc, xT, w, gate, offs, pos1, pos2, out):
                         start=(g == 0),
                         stop=(g == PASSES - 1),
                     )
-                nc.scalar.copy(sums[m][:, e * C : (e + 1) * C], acc[:])
+                if not together:
+                    nc.scalar.copy(sums[m][:, e * C : (e + 1) * C], acc)
+            if together:
+                nc.scalar.copy(sums[m][:, experts[0] * C : (experts[-1] + 1) * C], bank[:])
 
-        multiply(0, (0, 1), w_b0_e01)
+        multiply(0, (0, 1), w_b0_e01, together=True)
         multiply(0, (2, 3), w_b0_e23)
         multiply(1, (0,), w_b1_e0)
         multiply(1, (1, 2), w_b1_e12)

@@ -195,8 +195,8 @@ def tile_routed_moe_kernel(tc, xT, w, gate, offs, pos1, pos2, out):
         staged_b0_e01 = stage_weights("staged_b0_e01", "staged_b0_e01", 2)
         interleave_weights("gpsimd", staged_b0_e01, 0, 0, 0, 1)
         interleave_weights("gpsimd", staged_b0_e01, 1, 0, 1, 1)
-        staged_b1_e0 = stage_weights("staged_b1_e0", "staged_b1_e0", 1)
-        interleave_weights("gpsimd", staged_b1_e0, 0, 1, 0, 1)
+        staged_b1 = keep.tile([P, E * PASSES, P, PACK], BF16, name="staged_b1", align_bytes=64)
+        interleave_weights("gpsimd", staged_b1, 0, 1, 0, 1)
 
         codes01 = keep.tile([P, PASSES, PAIR * C], U32, name="codes01", align_bytes=64)
         quantize_tokens(codes01[:].rearrange("p g c -> p (g c)"), 0, PAIR * PASSES)
@@ -204,13 +204,12 @@ def tile_routed_moe_kernel(tc, xT, w, gate, offs, pos1, pos2, out):
 
         staged_b0_e23 = placed.tile([P, 8, P, PACK], BF16, name="staged_b0_e23", offset=0, align_bytes=64)
         interleave_weights("vector", staged_b0_e23, 0, 0, 2, 2)
-        staged_b1_e123 = keep.tile([P, 3 * PASSES, P, PACK], BF16, name="staged_b1_e123", align_bytes=64)
         nc.vector.tensor_copy(
-            staged_b1_e123[:, 4:6, :, :].rearrange("p u (c i) j -> p u c j i", i=RUN),
+            staged_b1[:, 6:8, :, :].rearrange("p u (c i) j -> p u c j i", i=RUN),
             w_raw[:, 6:8, :, P : 2 * P].rearrange("p u j (c i) -> p u c j i", i=RUN),
         )
         nc.vector.tensor_copy(
-            staged_b1_e123[:, 3, :, :].rearrange("p (c i) j -> p c j i", i=RUN),
+            staged_b1[:, 5, :, :].rearrange("p (c i) j -> p c j i", i=RUN),
             w_raw[:, 5, :, P : 2 * P].rearrange("p j (c i) -> p c j i", i=RUN),
         )
         w_b0_e23 = quantize_weights("w_b0_e23", "w_b0_e23", staged_b0_e23, 2)
@@ -222,13 +221,11 @@ def tile_routed_moe_kernel(tc, xT, w, gate, offs, pos1, pos2, out):
             quantize_tokens(codes23_runs[:, at * C : (at + PASSES) * C], PAIR * PASSES + at, PASSES)
 
         nc.scalar.copy(
-            staged_b1_e123[:, 0:3, :, :].rearrange("p u (c i) j -> p u c j i", i=RUN),
+            staged_b1[:, 2:5, :, :].rearrange("p u (c i) j -> p u c j i", i=RUN),
             w_raw[:, 2:5, :, P : 2 * P].rearrange("p u j (c i) -> p u c j i", i=RUN),
         )
 
-        w_b1_e3 = quantize_weights("w_b1_e3", "", staged_b1_e123[:, 4:6, :, :], 1, at_byte=7168)
-        w_b1_e0 = quantize_weights("w_b1_e0", "", staged_b1_e0, 1, at_byte=4096)
-        w_b1_e12 = quantize_weights("w_b1_e12", "", staged_b1_e123, 2, at_byte=5120)
+        w_b1 = quantize_weights("w_b1", "", staged_b1, E, at_byte=4096)
 
         def token_operand(e, g):
             if e < PAIR:
@@ -262,9 +259,7 @@ def tile_routed_moe_kernel(tc, xT, w, gate, offs, pos1, pos2, out):
 
         multiply(0, (0, 1), w_b0_e01, together=True)
         multiply(0, (2, 3), w_b0_e23)
-        multiply(1, (0,), w_b1_e0)
-        multiply(1, (1, 2), w_b1_e12)
-        multiply(1, (3,), w_b1_e3)
+        multiply(1, (0, 1, 2, 3), w_b1)
 
         def fetch(part, m, r, t0, t1):
             nc.vector.tensor_tensor(

@@ -214,6 +214,16 @@ def tile_routed_moe_kernel(tc, xT, w, gate, offs, pos1, pos2, out):
         )
         w_b0_e23 = quantize_weights("w_b0_e23", "w_b0_e23", staged_b0_e23, 2)
 
+        warm = psum.tile([P, T], F32, name="warm")
+        for i in range(3):
+            nc.tensor.matmul(
+                warm[:],
+                lhsT=staged_b1[:, 7, 0 : P // PACK, :].rearrange("p n j -> p (n j)"),
+                rhs=staged_b1[:, 6, :, :].rearrange("p n j -> p (n j)"),
+                start=True,
+                stop=True,
+            )
+
         codes23 = placed.tile([P, PASSES, PAIR * C], U32, name="codes23", offset=0, align_bytes=64)
         codes23_runs = codes23[:].rearrange("p g c -> p (g c)")
         for e in range(PAIR, E):

@@ -92,8 +92,7 @@ def tile_routed_moe_kernel(tc, xT, w, gate, offs, pos1, pos2, out):
                 nc.sync.dma_start(gate_t[(r, m)][:], gate[r, m * P : (m + 1) * P, :])
 
         cast1 = keep.tile([P, PACK, T], BF16, name="cast1", tag="cast1", align_bytes=64)
-        nc.scalar.copy(cast1[:, 0, :], planes1[:, 0, :])
-        for t in range(1, PACK):
+        for t in range(PACK):
             nc.gpsimd.tensor_copy(cast1[:, t, :], planes1[:, t, :])
 
         sums = [keep.tile([P, E * C], F32, name="sums%d" % m) for m in range(BLOCKS)]

@@ -191,11 +191,14 @@ def tile_routed_moe_kernel(tc, xT, w, gate, offs, pos1, pos2, out):
                 in_=tokens[:].rearrange("p q g c t -> p (q g c t)")[:, first * C * PACK : (first + runs) * C * PACK],
             )
 
-        staged_b0_e01 = stage_weights("staged_b0_e01", "staged_b0_e01", 2)
-        interleave_weights("gpsimd", staged_b0_e01, 0, 0, 0, 1)
+        staged_all = keep.tile([P, 12, P, PACK], BF16, name="staged_all", align_bytes=64)
+        staged_b0_e01 = staged_all[:, 0:4, :, :]
+        staged_b1 = staged_all[:, 4:12, :, :]
+        for g in range(PASSES):
+            nc.gpsimd.tensor_copy(
+                staged_all[:, g : g + 5 : 4, :, :], w_raw[:, g, :, :].rearrange("p j (m n) -> p m n j", m=BLOCKS)
+            )
         interleave_weights("gpsimd", staged_b0_e01, 1, 0, 1, 1)
-        staged_b1 = keep.tile([P, E * PASSES, P, PACK], BF16, name="staged_b1", align_bytes=64)
-        interleave_weights("gpsimd", staged_b1, 0, 1, 0, 1)
 
         codes01 = keep.tile([P, PASSES, PAIR * C], U32, name="codes01", align_bytes=64)
         quantize_tokens(codes01[:].rearrange("p g c -> p (g c)"), 0, PAIR * PASSES)

@@ -194,11 +194,13 @@ def tile_routed_moe_kernel(tc, xT, w, gate, offs, pos1, pos2, out):
         staged_all = keep.tile([P, 12, P, PACK], BF16, name="staged_all", align_bytes=64)
         staged_b0_e01 = staged_all[:, 0:4, :, :]
         staged_b1 = staged_all[:, 4:12, :, :]
-        for g in range(PASSES):
+        for u in range(3):
             nc.gpsimd.tensor_copy(
-                staged_all[:, g : g + 5 : 4, :, :], w_raw[:, g, :, :].rearrange("p j (m n) -> p m n j", m=BLOCKS)
+                staged_all[:, u : u + 5 : 4, :, :], w_raw[:, u, :, :].rearrange("p j (m n) -> p m n j", m=BLOCKS)
             )
-        interleave_weights("gpsimd", staged_b0_e01, 1, 0, 1, 1)
+        nc.gpsimd.tensor_copy(
+            staged_all[:, 3:4, :, :], w_raw[:, 3:4, :, 0:P].rearrange("p u j n -> p u n j")
+        )
 
         codes01 = keep.tile([P, PASSES, PAIR * C], U32, name="codes01", align_bytes=64)
         quantize_tokens(codes01[:].rearrange("p g c -> p (g c)"), 0, PAIR * PASSES)
@@ -209,10 +211,6 @@ def tile_routed_moe_kernel(tc, xT, w, gate, offs, pos1, pos2, out):
         nc.vector.tensor_copy(
             staged_b1[:, 6:8, :, :].rearrange("p u (c i) j -> p u c j i", i=RUN),
             w_raw[:, 6:8, :, P : 2 * P].rearrange("p u j (c i) -> p u c j i", i=RUN),
-        )
-        nc.vector.tensor_copy(
-            staged_b1[:, 5, :, :].rearrange("p (c i) j -> p c j i", i=RUN),
-            w_raw[:, 5, :, P : 2 * P].rearrange("p j (c i) -> p c j i", i=RUN),
         )
         w_b0_e23 = quantize_weights("w_b0_e23", "w_b0_e23", staged_b0_e23, 2)
 
@@ -233,8 +231,8 @@ def tile_routed_moe_kernel(tc, xT, w, gate, offs, pos1, pos2, out):
             quantize_tokens(codes23_runs[:, at * C : (at + PASSES) * C], PAIR * PASSES + at, PASSES)
 
         nc.scalar.copy(
-            staged_b1[:, 2:5, :, :].rearrange("p u (c i) j -> p u c j i", i=RUN),
-            w_raw[:, 2:5, :, P : 2 * P].rearrange("p u j (c i) -> p u c j i", i=RUN),
+            staged_b1[:, 3:6, :, :].rearrange("p u (c i) j -> p u c j i", i=RUN),
+            w_raw[:, 3:6, :, P : 2 * P].rearrange("p u j (c i) -> p u c j i", i=RUN),
         )
 
         w_b1 = quantize_weights("w_b1", "", staged_b1, E, at_byte=4096)

@@ -207,7 +207,8 @@ def tile_routed_moe_kernel(tc, xT, w, gate, offs, pos1, pos2, out):
         w_b0_e01 = quantize_weights("w_b0_e01", "w_b0_e01", staged_b0_e01, 2)
 
         staged_b0_e23 = placed.tile([P, 8, P, PACK], BF16, name="staged_b0_e23", offset=0, align_bytes=64)
-        interleave_weights("vector", staged_b0_e23, 0, 0, 2, 2)
+        interleave_weights("vector", staged_b0_e23, 0, 0, 2, 1)
+        interleave_weights("vector", staged_b0_e23, 1, 0, 3, 1)
         nc.vector.tensor_copy(
             staged_b1[:, 6:8, :, :].rearrange("p u (c i) j -> p u c j i", i=RUN),
             w_raw[:, 6:8, :, P : 2 * P].rearrange("p u j (c i) -> p u c j i", i=RUN),

@@ -41,9 +41,9 @@ def tile_routed_moe_kernel(tc, xT, w, gate, offs, pos1, pos2, out):
         placed = ctx.enter_context(tc.tile_pool(name="placed", bufs=1))
 
         offs_t = lists.tile([P, E * LIST_COLS], U16, name="offs_t")
-        planes0 = [keep.tile([P, T], F32, name="plane0_%d" % t) for t in range(PACK)]
-        planes1 = keep.tile([P, PACK, T], F32, name="planes1")
-        w_raw = keep.tile([P, E * PASSES, PACK, N], F32, name="w_raw")
+        planes0 = [keep.tile([P, T], F32, name="plane0_%d" % t, align_bytes=256) for t in range(PACK)]
+        planes1 = keep.tile([P, PACK, T], F32, name="planes1", align_bytes=256)
+        w_raw = keep.tile([P, E * PASSES, PACK, N], F32, name="w_raw", align_bytes=256)
         x_view = xT.rearrange("(g p t) n -> g p t n", p=P, t=PACK)
 
         def load_plane0(t):
@@ -88,7 +88,7 @@ def tile_routed_moe_kernel(tc, xT, w, gate, offs, pos1, pos2, out):
         gate_t = {}
         for m in range(BLOCKS):
             for r in range(ROUTES):
-                gate_t[(r, m)] = keep.tile([P, T], F32, name="gate%d_%d" % (r, m))
+                gate_t[(r, m)] = keep.tile([P, T], F32, name="gate%d_%d" % (r, m), align_bytes=256)
                 nc.sync.dma_start(gate_t[(r, m)][:], gate[r, m * P : (m + 1) * P, :])
 
         cast1 = keep.tile([P, PACK, T], BF16, name="cast1", tag="cast1", align_bytes=64)
@@ -285,7 +285,7 @@ def tile_routed_moe_kernel(tc, xT, w, gate, offs, pos1, pos2, out):
         for r in range(ROUTES):
             parts0.append(keep.tile([P, T], F32, name="part%d_0" % r))
             fetch(parts0[r], 0, r, 0, T)
-        result0 = keep.tile([P, T], F32, name="result0", tag="gate0_1")
+        result0 = keep.tile([P, T], F32, name="result0", tag="gate0_1", align_bytes=256)
         add_and_store(result0, parts0, 0, 0, T)
 
         parts1 = [keep.tile([P, T], F32, name="part0_1")]
@@ -293,6 +293,6 @@ def tile_routed_moe_kernel(tc, xT, w, gate, offs, pos1, pos2, out):
         parts1.append(keep.tile([P, T], F32, name="part1_1"))
         for t0 in (0, HALF):
             fetch(parts1[1], 1, 1, t0, t0 + HALF)
-        result1 = keep.tile([P, T], F32, name="result1")
+        result1 = keep.tile([P, T], F32, name="result1", align_bytes=256)
         for t0 in (0, HALF):
             add_and_store(result1, parts1, 1, t0, t0 + HALF)

@@ -207,8 +207,7 @@ def tile_routed_moe_kernel(tc, xT, w, gate, offs, pos1, pos2, out):
         w_b0_e01 = quantize_weights("w_b0_e01", "w_b0_e01", staged_b0_e01, 2)
 
         staged_b0_e23 = placed.tile([P, 8, P, PACK], BF16, name="staged_b0_e23", offset=0, align_bytes=64)
-        interleave_weights("vector", staged_b0_e23, 0, 0, 2, 1)
-        interleave_weights("vector", staged_b0_e23, 1, 0, 3, 1)
+        interleave_weights("vector", staged_b0_e23, 0, 0, 2, 2)
         nc.vector.tensor_copy(
             staged_b1[:, 6:8, :, :].rearrange("p u (c i) j -> p u c j i", i=RUN),
             w_raw[:, 6:8, :, P : 2 * P].rearrange("p u j (c i) -> p u c j i", i=RUN),

from contextlib import ExitStack

import concourse.mybir as mybir

K, T, E, C, N = 1024, 512, 4, 256, 256
FLOPS = 2 * K * N * E * C

F32 = mybir.dt.float32
BF16 = mybir.dt.bfloat16
U32 = mybir.dt.uint32
U16 = mybir.dt.uint16
U8 = mybir.dt.uint8
FP8X4 = mybir.dt.float8_e4m3fn_x4
MULT = mybir.AluOpType.mult
ADD = mybir.AluOpType.add
COPY = mybir.ActivationFunctionType.Copy

P = 128
PACK = 4
K_PASS = P * PACK
PASSES = K // K_PASS
BLOCKS = N // P
PAIR = 2
PAIRS = E // PAIR
WORD = 2
WINDOW = 2 * T
LIST_UNIT = 16
LIST_COLS = C // LIST_UNIT
RUN = 4
HALF = T // 2
ROUTES = 2


def tile_routed_moe_kernel(tc, xT, w, gate, offs, pos1, pos2, out):
    nc = tc.nc

    with ExitStack() as ctx:
        lists = ctx.enter_context(tc.tile_pool(name="lists", bufs=1))
        keep = ctx.enter_context(tc.tile_pool(name="keep", bufs=1))
        psum = ctx.enter_context(tc.psum_pool(name="psum", bufs=1))
        placed = ctx.enter_context(tc.tile_pool(name="placed", bufs=1))

        offs_t = lists.tile([P, E * LIST_COLS], U16, name="offs_t")
        planes0 = [keep.tile([P, T], F32, name="plane0_%d" % t, align_bytes=256) for t in range(PACK)]
        planes1 = keep.tile([P, PACK, T], F32, name="planes1", align_bytes=256)
        w_raw = keep.tile([P, E * PASSES, PACK, N], F32, name="w_raw", align_bytes=256)
        x_view = xT.rearrange("(g p t) n -> g p t n", p=P, t=PACK)

        def load_plane0(t):
            nc.sync.dma_start(planes0[t][:, 0:T], x_view[0, :, t, :])

        def load_plane1(t):
            nc.sync.dma_start(planes1[:, t, :], x_view[1, :, t, :])

        def load_weights(e):
            nc.sync.dma_start(
                w_raw[:, e * PASSES : (e + 1) * PASSES, :, :].rearrange("p g j n -> p g (j n)"),
                w[e].rearrange("(g p j) n -> p g (j n)", p=P, j=PACK),
            )

        def load_weights_of_pass(e, g):
            nc.sync.dma_start(
                w_raw[:, e * PASSES + g, :, :], w[e, g * K_PASS : (g + 1) * K_PASS, :].rearrange("(p j) n -> p j n", j=PACK)
            )

        load_plane0(0)
        nc.sync.dma_start(offs_t[:], offs)
        load_plane1(0)
        load_plane0(1)
        load_plane1(1)
        load_plane1(2)
        load_weights_of_pass(0, 0)
        load_plane1(3)
        load_plane0(2)
        load_weights_of_pass(0, 1)
        load_weights_of_pass(1, 0)
        load_plane0(3)
        load_weights_of_pass(1, 1)
        load_weights(2)
        load_weights(3)

        pos1_t = lists.tile([P, T // LIST_UNIT], U16, name="pos1_t")
        nc.sync.dma_start(pos1_t[:], pos1)
        pos2_t = lists.tile([P, T // LIST_UNIT], U16, name="pos2_t")
        nc.sync.dma_start(pos2_t[:], pos2)
        pos_t = (pos1_t, pos2_t)

        gate_t = {}
        for m in range(BLOCKS):
            for r in range(ROUTES):
                gate_t[(r, m)] = keep.tile([P, T], F32, name="gate%d_%d" % (r, m), align_bytes=256)
                nc.sync.dma_start(gate_t[(r, m)][:], gate[r, m * P : (m + 1) * P, :])

        cast1 = keep.tile([P, PACK, T], BF16, name="cast1", tag="cast1", align_bytes=64)
        for t in range(PACK):
            nc.gpsimd.tensor_copy(cast1[:, t, :], planes1[:, t, :])

        sums = [keep.tile([P, E * C], F32, name="sums%d" % m) for m in range(BLOCKS)]

        tokens = keep.tile([P, PAIRS, PASSES, PAIR * C, PACK], BF16, name="tokens", tag="tokens", align_bytes=64)
        token_scales = keep.tile([P, PAIRS, PASSES, PAIR * C], U8, name="token_scales", align_bytes=64)
        runs23 = tokens[:, 1, :, :, :].rearrange("p g c t -> p (g c t)").rearrange("p (b c t) -> p b c t", b=PAIR * PASSES, t=PACK)
        run_of = {(2, 1): 0, (2, 0): 1, (3, 0): 2, (3, 1): 3}

        pairs0 = [keep.tile([P, PACK // WORD, PAIR * C, WORD], BF16, name="pairs0_%d" % q, align_bytes=64) for q in range(PAIRS)]
        for t in range(PACK):
            for e in range(E):
                a = (e % PAIR) * C
                nc.vector.tensor_copy(
                    pairs0[e // PAIR][:, t // WORD, a : a + C, t % WORD],
                    planes0[t][:].indirect(offs_t[:, e * LIST_COLS : (e + 1) * LIST_COLS]),
                )

        pairs1 = {}

        def pairs_tile(e):
            pairs1[e] = keep.tile([P, PACK // WORD, C, WORD], BF16, name="pairs1_%d" % e, tag="pairs1_%d" % (e % PAIR), align_bytes=64)

        def gather1(e, t):
            nc.scalar.activation(
                pairs1[e][:, t // WORD, :, t % WORD], cast1[:, t, :].indirect(offs_t[:, e * LIST_COLS : (e + 1) * LIST_COLS]), COPY
            )

        def weave1(e):
            run = tokens[:, 0, 1, e * C : (e + 1) * C, :] if e < PAIR else runs23[:, run_of[(e, 1)], :, :]
            nc.scalar.copy(
                run.rearrange("p c t -> p (c t)").bitcast(F32).rearrange("p (c h) -> p c h", h=PACK // WORD),
                pairs1[e][:].rearrange("p h c e -> p (h c e)").bitcast(F32).rearrange("p (h c) -> p c h", h=PACK // WORD),
            )

        pairs_tile(0)
        pairs_tile(1)
        for t in range(PACK):
            gather1(0, t)
            gather1(1, t)
        weave1(0)
        weave1(1)
        pairs_tile(2)
        pairs_tile(3)
        for t in (0, 2, 1, 3):
            gather1(2, t)
        gather1(3, 0)
        weave1(2)
        for t in (2, 1, 3):
            gather1(3, t)
        weave1(3)

        def weave0(q, run):
            nc.vector.tensor_copy(
                run.bitcast(F32).rearrange("p (c h) -> p c h", h=PACK // WORD),
                pairs0[q][:].rearrange("p h c e -> p (h c e)").bitcast(F32).rearrange("p (h c) -> p c h", h=PACK // WORD),
            )

        weave0(0, tokens[:, 0, 0, :, :].rearrange("p c t -> p (c t)"))
        weave0(1, runs23[:, run_of[(2, 0)] : run_of[(3, 0)] + 1, :, :].rearrange("p b c t -> p (b c t)"))

        def stage_weights(name, tag, experts):
            return keep.tile([P, experts * PASSES, P, PACK], BF16, name=name, tag=tag, align_bytes=64)

        def interleave_weights(engine, staged, at, m, e, experts):
            src = w_raw[:, e * PASSES : (e + experts) * PASSES, :, m * P : (m + 1) * P]
            dst = staged[:, at * PASSES : (at + experts) * PASSES, :, :]
            if engine == "gpsimd":
                for u in range(experts * PASSES):
                    nc.gpsimd.tensor_copy(dst[:, u : u + 1, :, :], src[:, u : u + 1, :, :].rearrange("p u j n -> p u n j"))
                return
            dst = dst.rearrange("p u (c i) j -> p u c j i", i=RUN)
            src = src.rearrange("p u j (c i) -> p u c j i", i=RUN)
            if engine == "scalar":
                nc.scalar.copy(dst, src)
            else:
                nc.vector.tensor_copy(dst, src)

        def quantize_weights(name, tag, staged, experts, at_byte=None):
            if at_byte is None:
                codes = keep.tile([P, experts * PASSES, P], U32, name=name + "_codes", tag=tag, align_bytes=64)
            else:
                codes = placed.tile([P, experts * PASSES, P], U32, name=name + "_codes", offset=at_byte, align_bytes=64)
            scales = keep.tile([P, experts * PASSES, P], U8, name=name + "_scales", align_bytes=64)
            nc.vector.quantize_mx(
                out=codes[:].rearrange("p u n -> p (u n)").bitcast(FP8X4),
                scales=scales[:].rearrange("p u n -> p (u n)"),
                in_=staged[:, 0 : experts * PASSES, :, :].rearrange("p u n j -> p (u n j)"),
            )
            return codes, scales

        def quantize_tokens(codes, first, runs):
            nc.vector.quantize_mx(
                out=codes.bitcast(FP8X4),
                scales=token_scales[:].rearrange("p q g c -> p (q g c)")[:, first * C : (first + runs) * C],
                in_=tokens[:].rearrange("p q g c t -> p (q g c t)")[:, first * C * PACK : (first + runs) * C * PACK],
            )

        staged_all = keep.tile([P, 12, P, PACK], BF16, name="staged_all", align_bytes=64)
        staged_b0_e01 = staged_all[:, 0:4, :, :]
        staged_b1 = staged_all[:, 4:12, :, :]
        for u in range(3):
            nc.gpsimd.tensor_copy(
                staged_all[:, u : u + 5 : 4, :, :], w_raw[:, u, :, :].rearrange("p j (m n) -> p m n j", m=BLOCKS)
            )
        nc.gpsimd.tensor_copy(
            staged_all[:, 3:4, :, :], w_raw[:, 3:4, :, 0:P].rearrange("p u j n -> p u n j")
        )

        codes01 = keep.tile([P, PASSES, PAIR * C], U32, name="codes01", align_bytes=64)
        quantize_tokens(codes01[:].rearrange("p g c -> p (g c)"), 0, PAIR * PASSES)
        w_b0_e01 = quantize_weights("w_b0_e01", "w_b0_e01", staged_b0_e01, 2)

        staged_b0_e23 = placed.tile([P, 8, P, PACK], BF16, name="staged_b0_e23", offset=0, align_bytes=64)
        interleave_weights("vector", staged_b0_e23, 0, 0, 2, 2)
        nc.vector.tensor_copy(
            staged_b1[:, 6:8, :, :].rearrange("p u (c i) j -> p u c j i", i=RUN),
            w_raw[:, 6:8, :, P : 2 * P].rearrange("p u j (c i) -> p u c j i", i=RUN),
        )
        w_b0_e23 = quantize_weights("w_b0_e23", "w_b0_e23", staged_b0_e23, 2)

        warm = psum.tile([P, T], F32, name="warm")
        for i in range(3):
            nc.tensor.matmul(
                warm[:],
                lhsT=staged_b1[:, 7, 0 : P // PACK, :].rearrange("p n j -> p (n j)"),
                rhs=staged_b1[:, 6, :, :].rearrange("p n j -> p (n j)"),
                start=True,
                stop=True,
            )

        codes23 = placed.tile([P, PASSES, PAIR * C], U32, name="codes23", offset=0, align_bytes=64)
        codes23_runs = codes23[:].rearrange("p g c -> p (g c)")
        for e in range(PAIR, E):
            at = (e - PAIR) * PASSES
            quantize_tokens(codes23_runs[:, at * C : (at + PASSES) * C], PAIR * PASSES + at, PASSES)

        nc.scalar.copy(
            staged_b1[:, 3:6, :, :].rearrange("p u (c i) j -> p u c j i", i=RUN),
            w_raw[:, 3:6, :, P : 2 * P].rearrange("p u j (c i) -> p u c j i", i=RUN),
        )

        w_b1 = quantize_weights("w_b1", "", staged_b1, E, at_byte=4096)

        def token_operand(e, g):
            if e < PAIR:
                return codes01[:, g, e * C : (e + 1) * C], token_scales[:, 0, g, e * C : (e + 1) * C]
            b = run_of[(e, g)]
            return (
                codes23_runs[:, b * C : (b + 1) * C],
                token_scales[:, 1, :, :].rearrange("p g c -> p (g c)")[:, b * C : (b + 1) * C],
            )

        def multiply(m, experts, piece, together=False):
            codes, scales = piece
            bank = psum.tile([P, len(experts) * C], F32, name="bank%d_%d" % (experts[0], m)) if together else None
            for i, e in enumerate(experts):
                acc = bank[:, i * C : (i + 1) * C] if together else psum.tile([P, C], F32, name="acc%d_%d" % (e, m))[:]
                for g in range(PASSES):
                    rhs, rhs_scale = token_operand(e, g)
                    nc.tensor.matmul_mx(
                        out=acc,
                        lhsT=codes[:, i * PASSES + g, :].bitcast(FP8X4),
                        lhsT_scale=scales[:, i * PASSES + g, :],
                        rhs=rhs.bitcast(FP8X4),
                        rhs_scale=rhs_scale,
                        start=(g == 0),
                        stop=(g == PASSES - 1),
                    )
                if not together:
                    nc.scalar.copy(sums[m][:, e * C : (e + 1) * C], acc)
            if together:
                nc.scalar.copy(sums[m][:, experts[0] * C : (experts[-1] + 1) * C], bank[:])

        multiply(0, (0, 1), w_b0_e01, together=True)
        multiply(0, (2, 3), w_b0_e23)
        multiply(1, (0, 1, 2, 3), w_b1)

        def fetch(part, m, r, t0, t1):
            nc.vector.tensor_tensor(
                part[:, t0:t1], sums[m][:].indirect(pos_t[r][:, t0 // LIST_UNIT : t1 // LIST_UNIT]), gate_t[(r, m)][:, t0:t1], MULT
            )

        def add_and_store(result, parts, m, t0, t1):
            nc.vector.tensor_tensor(result[:, t0:t1], parts[0][:, t0:t1], parts[1][:, t0:t1], ADD)
            nc.sync.dma_start(out[m * P : (m + 1) * P, t0:t1], result[:, t0:t1])

        parts0 = []
        for r in range(ROUTES):
            parts0.append(keep.tile([P, T], F32, name="part%d_0" % r))
            fetch(parts0[r], 0, r, 0, T)
        result0 = keep.tile([P, T], F32, name="result0", tag="gate0_1", align_bytes=256)
        add_and_store(result0, parts0, 0, 0, T)

        parts1 = [keep.tile([P, T], F32, name="part0_1")]
        fetch(parts1[0], 1, 0, 0, T)
        parts1.append(keep.tile([P, T], F32, name="part1_1"))
        for t0 in (0, HALF):
            fetch(parts1[1], 1, 1, t0, t0 + HALF)
        result1 = keep.tile([P, T], F32, name="result1", align_bytes=256)
        for t0 in (0, HALF):
            add_and_store(result1, parts1, 1, t0, t0 + HALF)
